import numpy as np
import ml_dtypes


def mxq(x, axis, fmt="e4m3"):
    dtype, down = {"e4m3": (ml_dtypes.float8_e4m3fn, 7), "e5m2": (ml_dtypes.float8_e5m2, 14)}[fmt]
    v = np.moveaxis(np.asarray(x, np.float32).astype(ml_dtypes.bfloat16).astype(np.float64), axis, -1)
    blocks = v.reshape(v.shape[:-1] + (-1, 32))
    amax = np.abs(blocks).max(-1, keepdims=True)
    byte = np.maximum(np.where(amax > 0, np.frexp(amax)[1] - 1 + 127, 0) - down, 1)
    scale = np.exp2(byte - 127.0)
    codes = (blocks / scale).astype(np.float32).astype(dtype).astype(np.float64)
    return np.moveaxis((codes * scale).reshape(v.shape), -1, axis)


WIDE = False


def mx_kscale(k):
    if not WIDE:
        return np.ones(k)
    levels = np.array([10, -10, 5, -5, 0])
    if k % 512:
        return np.exp2(np.random.permutation(np.resize(levels, k // 32))).repeat(32)
    a = np.empty((k // 512, 16))
    for p in range(k // 512):
        a[p, :8] = np.random.permutation(np.resize(levels, 8))
        for g in range(8):
            far = levels[np.abs(levels - a[p, g]) >= 10]
            a[p, g + 8] = far[np.random.randint(len(far))]
    return np.exp2(a.ravel()).repeat(32)


def f64(x):
    return np.asarray(x).astype(np.float64)


def striped(idx):
    return np.tile(idx.reshape(-1, 16).T, (8, 1)).astype(np.uint16)


def unstriped(offs):
    return offs[:16].T.reshape(-1).astype(np.int64)


def pack_weight(w):
    k, n = w.shape
    w = f64(np.asarray(w, np.float32).astype(ml_dtypes.bfloat16)).reshape(k // 32, 32, n)
    amax = np.abs(w).max(1)
    byte = np.clip(np.where(amax > 0, np.frexp(amax)[1] - 1 + 127 - 7, 1), 1, 254)
    scaled = (w * np.exp2(127.0 - byte)[:, None, :]).reshape(k, n).astype(np.float32)
    words = np.ascontiguousarray(scaled.reshape(k // 512, 128, 4, n).transpose(0, 1, 3, 2)).astype(ml_dtypes.float8_e4m3fn).view(np.uint8)
    return words, np.ascontiguousarray(byte.astype(np.uint8).reshape(k // 512, 16, n))


def unpack_weight(words, scales):
    g, p, n, _ = words.shape
    vals = np.ascontiguousarray(words).view(ml_dtypes.float8_e4m3fn).astype(np.float64) * np.repeat(np.exp2(scales.astype(np.float64) - 127.0), 8, axis=1)[..., None]
    return vals.transpose(0, 1, 3, 2).reshape(g * 512, n)


def sigmoid(v):
    return 1.0 / (1.0 + np.exp(-np.maximum(v, -700.0)))


K, T, S, N, D = 512, 2048, 512, 128, 2
P = 2 ** 7


def setup_inputs():
    n = np.random.standard_normal
    s = mx_kscale(K)[:, None]
    packed_xT = pack_weight(n((K, T)) * s)
    return {
        "x_words": packed_xT[0],
        "x_scales": packed_xT[1],
        "w1": (n((K, N)) / np.sqrt(K) / s).astype(np.float32),
        "gate": (np.tile(np.random.uniform(0.3, 0.6, (D, 1, S)), (1, P, 1))).astype(np.float32),
        "goal": ((np.random.uniform(size=(N, S)) < 0.3) * 1.0).astype(np.float32),
        "known": (np.tile((np.random.uniform(size=S) < 0.5) * 1.0, (P, 1))).astype(np.float32),
        "offs": striped(np.random.permutation(T)[:S]),
        "pos1": striped(np.random.permutation(S)[:S]),
        "pos2": striped(np.random.permutation(S)[:S]),
    }


def reference(x_words, x_scales, w1, gate, goal, known, offs, pos1, pos2):
    xq = unpack_weight(x_words, x_scales)[:, unstriped(offs)]
    p = sigmoid(mxq(f64(w1), 0, "e4m3").T @ xq)
    ee = (f64(goal) - p) * f64(known)[:1]
    ss = ee[:, unstriped(pos1)] * f64(gate)[0, :1] + ee[:, unstriped(pos2)] * f64(gate)[1, :1]
    rr = ee + 0.8 * (ss[:, unstriped(pos1)] * f64(gate)[0, :1] + ss[:, unstriped(pos2)] * f64(gate)[1, :1])
    return p + 0.5 * rr

@@ -1,0 +1,100 @@
+from contextlib import ExitStack
+
+import concourse.mybir as mybir
+
+K, T, S, N = 512, 2048, 512, 128
+P = 128
+HALF = S // 2
+FLOPS = 2 * K * N * S
+
+F32 = mybir.dt.float32
+BF16 = mybir.dt.bfloat16
+I32 = mybir.dt.int32
+U32 = mybir.dt.uint32
+U16 = mybir.dt.uint16
+U8 = mybir.dt.uint8
+FP8X4 = mybir.dt.float8_e4m3fn_x4
+MULT = mybir.AluOpType.mult
+ADD = mybir.AluOpType.add
+SUB = mybir.AluOpType.subtract
+SIGMOID = mybir.ActivationFunctionType.Sigmoid
+
+
+def tile_picked_ycns_two_p_kernel(tc, x_words, x_scales, w1, gate, goal, known, offs, pos1, pos2, out):
+    nc = tc.nc
+    with ExitStack() as ctx:
+        keep = ctx.enter_context(tc.tile_pool(name="keep", bufs=1))
+        psum = ctx.enter_context(tc.psum_pool(name="psum", bufs=1))
+
+        offs_sb = keep.tile([P, S // 16], U16, name="offs_sb")
+        pos_sb = [keep.tile([P, S // 16], U16, name="pos%d_sb" % d) for d in range(2)]
+        table_words = keep.tile([P, T], I32, name="table_words", align_bytes=64)
+        table_scales = keep.tile([P, T], U8, name="table_scales", align_bytes=64)
+        w_raw = keep.tile([P, 4, N], F32, name="w_raw")
+        goal_sb = keep.tile([P, S], F32, name="goal_sb")
+        known_sb = keep.tile([P, S], F32, name="known_sb")
+        gate_sb = [keep.tile([P, S], F32, name="gate%d_sb" % d) for d in range(2)]
+
+        nc.vector.memset(table_scales[:].bitcast(I32), 0)
+        for q in range(4):
+            nc.scalar.dma_start(out=table_scales[32 * q:32 * q + 4, :].bitcast(I32),
+                                in_=x_scales[0, 4 * q:4 * q + 4, :].bitcast(I32))
+
+        nc.sync.dma_start(out=w_raw[:], in_=w1.rearrange("(p j) m -> p j m", j=4))
+        nc.sync.dma_start(offs_sb[:], offs)
+        nc.sync.dma_start(out=table_words[:], in_=x_words[0].rearrange("p n t -> p (n t)").bitcast(I32))
+        nc.sync.dma_start(out=goal_sb[:], in_=goal)
+        nc.sync.dma_start(out=known_sb[:], in_=known)
+        nc.sync.dma_start(pos_sb[0][:], pos1)
+        nc.sync.dma_start(pos_sb[1][:], pos2)
+        for d in range(2):
+            nc.sync.dma_start(out=gate_sb[d][:], in_=gate[d])
+
+        w_grouped = keep.tile([P, N, 4], BF16, name="w_grouped", align_bytes=64)
+        nc.vector.tensor_copy(out=w_grouped[:], in_=w_raw[:].rearrange("p j m -> p m j"))
+        picked_scales = keep.tile([P, S], U8, name="picked_scales", align_bytes=64)
+        nc.vector.tensor_copy(picked_scales[:], table_scales[:].indirect(offs_sb[:]))
+        w_codes = keep.tile([P, N], U32, name="w_codes", align_bytes=64)
+        w_scales = keep.tile([P, N], U8, name="w_scales", align_bytes=64)
+        nc.vector.quantize_mx(out=w_codes[:].bitcast(FP8X4), scales=w_scales[:],
+                              in_=w_grouped[:].rearrange("p m j -> p (m j)"))
+
+        cols = [slice(h * HALF, (h + 1) * HALF) for h in range(2)]
+        entries = [slice(h * HALF // 16, (h + 1) * HALF // 16) for h in range(2)]
+        p_sb = keep.tile([P, S], F32, name="p_sb")
+        for h in range(2):
+            picked_words = keep.tile([P, HALF], U32, name="picked_words%d" % h, align_bytes=64)
+            nc.vector.tensor_copy(picked_words[:], table_words[:].bitcast(U32).indirect(offs_sb[:, entries[h]]))
+            logits = psum.tile([P, HALF], F32, name="logits%d" % h)
+            nc.tensor.matmul_mx(out=logits[:], lhsT=w_codes[:].bitcast(FP8X4), lhsT_scale=w_scales[:],
+                                rhs=picked_words[:].bitcast(FP8X4), rhs_scale=picked_scales[:, cols[h]],
+                                start=True, stop=True)
+            nc.scalar.activation(p_sb[:, cols[h]], logits[:], SIGMOID)
+
+        miss = keep.tile([P, S], F32, name="miss")
+        ee = keep.tile([P, S], F32, name="ee")
+        for h in range(2):
+            nc.vector.tensor_tensor(miss[:, cols[h]], goal_sb[:, cols[h]], p_sb[:, cols[h]], SUB)
+            nc.vector.tensor_tensor(ee[:, cols[h]], miss[:, cols[h]], known_sb[:, cols[h]], MULT)
+
+        def weighted(window, d, h, name):
+            t = keep.tile([P, HALF], F32, name=name)
+            nc.vector.tensor_tensor(t[:], window[:].indirect(pos_sb[d][:, entries[h]]), gate_sb[d][:, cols[h]], MULT)
+            return t
+
+        ss = keep.tile([P, S], F32, name="ss")
+        first = [weighted(ee, 0, h, "first%d" % h) for h in range(2)]
+        second = [weighted(ee, 1, h, "second%d" % h) for h in range(2)]
+        for h in range(2):
+            nc.vector.tensor_tensor(ss[:, cols[h]], first[h][:], second[h][:], ADD)
+        base = keep.tile([P, S], F32, name="base")
+        nc.vector.scalar_tensor_tensor(base[:], ee[:], 0.5, p_sb[:], MULT, ADD)
+
+        for h in range(2):
+            third = weighted(ss, 0, h, "third%d" % h)
+            fourth = weighted(ss, 1, h, "fourth%d" % h)
+            part = keep.tile([P, HALF], F32, name="part%d" % h)
+            nc.vector.scalar_tensor_tensor(part[:], third[:], 0.4, base[:, cols[h]], MULT, ADD)
+            res = keep.tile([P, HALF], F32, name="res%d" % h)
+            nc.vector.scalar_tensor_tensor(res[:], fourth[:], 0.4, part[:], MULT, ADD)
+            nc.sync.dma_start(out=out[:, cols[h]], in_=res[:])

@@ -1,10 +1,14 @@
 from contextlib import ExitStack
 
 import concourse.mybir as mybir
+from concourse.masks import make_identity
 
 K, T, S, N = 512, 2048, 512, 128
 P = 128
+PACK = 4
+STRIPE = 16
 HALF = S // 2
+BLOCKS = S // P
 FLOPS = 2 * K * N * S
 
 F32 = mybir.dt.float32
@@ -18,6 +22,7 @@ MULT = mybir.AluOpType.mult
 ADD = mybir.AluOpType.add
 SUB = mybir.AluOpType.subtract
 SIGMOID = mybir.ActivationFunctionType.Sigmoid
+COPY = mybir.ActivationFunctionType.Copy
 
 
 def tile_picked_ycns_two_p_kernel(tc, x_words, x_scales, w1, gate, goal, known, offs, pos1, pos2, out):
@@ -26,22 +31,21 @@ def tile_picked_ycns_two_p_kernel(tc, x_words, x_scales, w1, gate, goal, known, 
         keep = ctx.enter_context(tc.tile_pool(name="keep", bufs=1))
         psum = ctx.enter_context(tc.psum_pool(name="psum", bufs=1))
 
-        offs_sb = keep.tile([P, S // 16], U16, name="offs_sb")
-        pos_sb = [keep.tile([P, S // 16], U16, name="pos%d_sb" % d) for d in range(2)]
+        offs_sb = keep.tile([P, S // STRIPE], U16, name="offs_sb")
+        pos_sb = [keep.tile([P, S // STRIPE], U16, name="pos%d_sb" % d) for d in range(2)]
         table_words = keep.tile([P, T], I32, name="table_words", align_bytes=64)
         table_scales = keep.tile([P, T], U8, name="table_scales", align_bytes=64)
-        w_raw = keep.tile([P, 4, N], F32, name="w_raw")
+        w_raw = keep.tile([P, PACK, N], F32, name="w_raw")
         goal_sb = keep.tile([P, S], F32, name="goal_sb")
         known_sb = keep.tile([P, S], F32, name="known_sb")
         gate_sb = [keep.tile([P, S], F32, name="gate%d_sb" % d) for d in range(2)]
 
         nc.vector.memset(table_scales[:].bitcast(I32), 0)
-        for q in range(4):
-            nc.scalar.dma_start(out=table_scales[32 * q:32 * q + 4, :].bitcast(I32),
-                                in_=x_scales[0, 4 * q:4 * q + 4, :].bitcast(I32))
-
-        nc.sync.dma_start(out=w_raw[:], in_=w1.rearrange("(p j) m -> p j m", j=4))
+        nc.sync.dma_start(out=w_raw[:], in_=w1.rearrange("(p j) m -> p j m", j=PACK))
         nc.sync.dma_start(offs_sb[:], offs)
+        for r in range(PACK):
+            queue = nc.sync if r < PACK // 2 else nc.scalar
+            queue.dma_start(out=table_scales[r:P:32, :].bitcast(I32), in_=x_scales[0, r:K // 32:PACK, :].bitcast(I32))
         nc.sync.dma_start(out=table_words[:], in_=x_words[0].rearrange("p n t -> p (n t)").bitcast(I32))
         nc.sync.dma_start(out=goal_sb[:], in_=goal)
         nc.sync.dma_start(out=known_sb[:], in_=known)
@@ -49,8 +53,10 @@ def tile_picked_ycns_two_p_kernel(tc, x_words, x_scales, w1, gate, goal, known, 
         nc.sync.dma_start(pos_sb[1][:], pos2)
         for d in range(2):
             nc.sync.dma_start(out=gate_sb[d][:], in_=gate[d])
+        ident = keep.tile([P, P], F32, name="ident")
+        make_identity(nc, ident[:])
 
-        w_grouped = keep.tile([P, N, 4], BF16, name="w_grouped", align_bytes=64)
+        w_grouped = keep.tile([P, N, PACK], BF16, name="w_grouped", align_bytes=64)
         nc.vector.tensor_copy(out=w_grouped[:], in_=w_raw[:].rearrange("p j m -> p m j"))
         picked_scales = keep.tile([P, S], U8, name="picked_scales", align_bytes=64)
         nc.vector.tensor_copy(picked_scales[:], table_scales[:].indirect(offs_sb[:]))
@@ -59,42 +65,66 @@ def tile_picked_ycns_two_p_kernel(tc, x_words, x_scales, w1, gate, goal, known, 
         nc.vector.quantize_mx(out=w_codes[:].bitcast(FP8X4), scales=w_scales[:],
                               in_=w_grouped[:].rearrange("p m j -> p (m j)"))
 
-        cols = [slice(h * HALF, (h + 1) * HALF) for h in range(2)]
-        entries = [slice(h * HALF // 16, (h + 1) * HALF // 16) for h in range(2)]
+        half = [slice(h * HALF, (h + 1) * HALF) for h in range(2)]
+        entries = [slice(h * HALF // STRIPE, (h + 1) * HALF // STRIPE) for h in range(2)]
+        block = [slice(b * P, (b + 1) * P) for b in range(BLOCKS)]
+
+        def bank(tag, name):
+            return psum.tile([P, S], F32, name=name, tag=tag)
+
         p_sb = keep.tile([P, S], F32, name="p_sb")
-        for h in range(2):
-            picked_words = keep.tile([P, HALF], U32, name="picked_words%d" % h, align_bytes=64)
-            nc.vector.tensor_copy(picked_words[:], table_words[:].bitcast(U32).indirect(offs_sb[:, entries[h]]))
-            logits = psum.tile([P, HALF], F32, name="logits%d" % h)
-            nc.tensor.matmul_mx(out=logits[:], lhsT=w_codes[:].bitcast(FP8X4), lhsT_scale=w_scales[:],
-                                rhs=picked_words[:].bitcast(FP8X4), rhs_scale=picked_scales[:, cols[h]],
-                                start=True, stop=True)
-            nc.scalar.activation(p_sb[:, cols[h]], logits[:], SIGMOID)
-
-        miss = keep.tile([P, S], F32, name="miss")
+        miss = keep.tile([P, S], F32, name="miss", tag="miss")
         ee = keep.tile([P, S], F32, name="ee")
+        picked_words = []
         for h in range(2):
-            nc.vector.tensor_tensor(miss[:, cols[h]], goal_sb[:, cols[h]], p_sb[:, cols[h]], SUB)
-            nc.vector.tensor_tensor(ee[:, cols[h]], miss[:, cols[h]], known_sb[:, cols[h]], MULT)
+            words = keep.tile([P, HALF], U32, name="picked_words%d" % h, align_bytes=64)
+            nc.vector.tensor_copy(words[:], table_words[:].bitcast(U32).indirect(offs_sb[:, entries[h]]))
+            picked_words.append(words)
+        for b in range(BLOCKS):
+            logits = bank("upright%d" % b, "logits%d" % b)
+            nc.tensor.matmul_mx(out=logits[:, 0:P], lhsT=w_codes[:].bitcast(FP8X4), lhsT_scale=w_scales[:],
+                                rhs=picked_words[b // 2][:, block[b % 2]].bitcast(FP8X4),
+                                rhs_scale=picked_scales[:, block[b]], start=True, stop=True)
+            nc.scalar.activation(p_sb[:, block[b]], logits[:, 0:P], SIGMOID)
+        for part in (half[0], block[2], block[3]):
+            nc.vector.tensor_tensor(miss[:, part], goal_sb[:, part], p_sb[:, part], SUB)
+            nc.vector.tensor_tensor(ee[:, part], miss[:, part], known_sb[:, part], MULT)
 
-        def weighted(window, d, h, name):
-            t = keep.tile([P, HALF], F32, name=name)
-            nc.vector.tensor_tensor(t[:], window[:].indirect(pos_sb[d][:, entries[h]]), gate_sb[d][:, cols[h]], MULT)
-            return t
+        def neighbours(window, d, weights, h, name):
+            weighted = keep.tile([P, HALF], F32, name=name)
+            nc.vector.tensor_tensor(weighted[:], window[:].indirect(pos_sb[d][:, entries[h]]), weights[:, half[h]], MULT)
+            return weighted
 
         ss = keep.tile([P, S], F32, name="ss")
-        first = [weighted(ee, 0, h, "first%d" % h) for h in range(2)]
-        second = [weighted(ee, 1, h, "second%d" % h) for h in range(2)]
+        ee_by_p0 = [neighbours(ee, 0, gate_sb[0], h, "ee_by_p0_%d" % h) for h in range(2)]
+        ee_by_p1 = [neighbours(ee, 1, gate_sb[1], h, "ee_by_p1_%d" % h) for h in range(2)]
         for h in range(2):
-            nc.vector.tensor_tensor(ss[:, cols[h]], first[h][:], second[h][:], ADD)
-        base = keep.tile([P, S], F32, name="base")
-        nc.vector.scalar_tensor_tensor(base[:], ee[:], 0.5, p_sb[:], MULT, ADD)
+            nc.vector.tensor_tensor(ss[:, half[h]], ee_by_p0[h][:], ee_by_p1[h][:], ADD)
 
-        for h in range(2):
-            third = weighted(ss, 0, h, "third%d" % h)
-            fourth = weighted(ss, 1, h, "fourth%d" % h)
-            part = keep.tile([P, HALF], F32, name="part%d" % h)
-            nc.vector.scalar_tensor_tensor(part[:], third[:], 0.4, base[:, cols[h]], MULT, ADD)
-            res = keep.tile([P, HALF], F32, name="res%d" % h)
-            nc.vector.scalar_tensor_tensor(res[:], fourth[:], 0.4, part[:], MULT, ADD)
-            nc.sync.dma_start(out=out[:, cols[h]], in_=res[:])
+        gate0_damped = keep.tile([P, S], F32, name="gate0_damped", tag="miss")
+        nc.scalar.activation(gate0_damped[:], gate_sb[0][:], COPY, scale=0.8)
+
+        turned = [bank("turned%d" % b, "turned%d" % b) for b in range(BLOCKS)]
+        for b in range(BLOCKS):
+            for i, term in enumerate((ee, p_sb, p_sb)):
+                nc.tensor.matmul(turned[b][:, 0:P], term[:, block[b]], ident[:], is_transpose=True,
+                                 start=(i == 0), stop=False)
+
+        ss_by_p0 = [neighbours(ss, 0, gate0_damped, h, "ss_by_p0_%d" % h) for h in range(2)]
+        ss_by_p1 = [neighbours(ss, 1, gate_sb[1], h, "ss_by_p1_%d" % h) for h in range(2)]
+        halved = keep.tile([P, S], F32, name="halved")
+        back = [bank("upright%d" % i, "back%d" % i) for i in range(3)]
+        partial = [back[0][:, block[0]], back[0][:, block[1]], back[1][:, 0:P], back[2][:, 0:P]]
+        for b in range(BLOCKS):
+            nc.tensor.matmul(turned[b][:, 0:P], ss_by_p0[b // 2][:, block[b % 2]], ident[:], is_transpose=True,
+                             start=False, stop=True)
+            nc.scalar.activation(halved[:, block[b]], turned[b][:, 0:P], COPY, scale=0.5)
+        for b in range(BLOCKS):
+            nc.tensor.transpose(partial[b], halved[:, block[b]], ident[:])
+
+        result = keep.tile([P, S], F32, name="result")
+        nc.vector.scalar_tensor_tensor(result[:, half[0]], ss_by_p1[0][:], 0.4, back[0][:, 0:HALF], MULT, ADD)
+        nc.sync.dma_start(out=out[:, half[0]], in_=result[:, half[0]])
+        for b, queue in ((2, nc.scalar), (3, nc.sync)):
+            nc.vector.scalar_tensor_tensor(result[:, block[b]], ss_by_p1[1][:, block[b % 2]], 0.4, partial[b], MULT, ADD)
+            queue.dma_start(out=out[:, block[b]], in_=result[:, block[b]])

@@ -66,65 +66,93 @@ def tile_picked_ycns_two_p_kernel(tc, x_words, x_scales, w1, gate, goal, known, 
                               in_=w_grouped[:].rearrange("p m j -> p (m j)"))
 
         half = [slice(h * HALF, (h + 1) * HALF) for h in range(2)]
-        entries = [slice(h * HALF // STRIPE, (h + 1) * HALF // STRIPE) for h in range(2)]
         block = [slice(b * P, (b + 1) * P) for b in range(BLOCKS)]
 
         def bank(tag, name):
             return psum.tile([P, S], F32, name=name, tag=tag)
 
+        def entries(listed, cols):
+            return listed[:, cols.start // STRIPE:cols.stop // STRIPE]
+
         p_sb = keep.tile([P, S], F32, name="p_sb")
-        miss = keep.tile([P, S], F32, name="miss", tag="miss")
+        miss = keep.tile([P, S], F32, name="miss")
         ee = keep.tile([P, S], F32, name="ee")
         picked_words = []
         for h in range(2):
             words = keep.tile([P, HALF], U32, name="picked_words%d" % h, align_bytes=64)
-            nc.vector.tensor_copy(words[:], table_words[:].bitcast(U32).indirect(offs_sb[:, entries[h]]))
+            nc.vector.tensor_copy(words[:], table_words[:].bitcast(U32).indirect(entries(offs_sb, half[h])))
             picked_words.append(words)
-        for b in range(BLOCKS):
-            logits = bank("upright%d" % b, "logits%d" % b)
-            nc.tensor.matmul_mx(out=logits[:, 0:P], lhsT=w_codes[:].bitcast(FP8X4), lhsT_scale=w_scales[:],
-                                rhs=picked_words[b // 2][:, block[b % 2]].bitcast(FP8X4),
-                                rhs_scale=picked_scales[:, block[b]], start=True, stop=True)
-            nc.scalar.activation(p_sb[:, block[b]], logits[:, 0:P], SIGMOID)
-        for part in (half[0], block[2], block[3]):
-            nc.vector.tensor_tensor(miss[:, part], goal_sb[:, part], p_sb[:, part], SUB)
-            nc.vector.tensor_tensor(ee[:, part], miss[:, part], known_sb[:, part], MULT)
+        products = [[0,128],[128,256],[256,384],[384,512]]
+        tags = ["upright0", "upright1", "upright2", "upright3", "back3", "back2"]
+        for i, (first, last) in enumerate(products):
+            logits = bank(tags[i], "logits%d" % i)
+            h = first // HALF
+            nc.tensor.matmul_mx(out=logits[:, 0:last - first], lhsT=w_codes[:].bitcast(FP8X4), lhsT_scale=w_scales[:],
+                                rhs=picked_words[h][:, first - h * HALF:last - h * HALF].bitcast(FP8X4),
+                                rhs_scale=picked_scales[:, first:last], start=True, stop=True)
+            nc.scalar.activation(p_sb[:, first:last], logits[:, 0:last - first], SIGMOID)
+        for op, first, last in [[0,0,256],[1,0,256],[0,256,384],[1,256,384],[0,384,512],[1,384,512]]:
+            part = slice(first, last)
+            if op == 0:
+                nc.vector.tensor_tensor(miss[:, part], goal_sb[:, part], p_sb[:, part], SUB)
+            else:
+                nc.vector.tensor_tensor(ee[:, part], miss[:, part], known_sb[:, part], MULT)
 
-        def neighbours(window, d, weights, h, name):
-            weighted = keep.tile([P, HALF], F32, name=name)
-            nc.vector.tensor_tensor(weighted[:], window[:].indirect(pos_sb[d][:, entries[h]]), weights[:, half[h]], MULT)
+        def neighbours_of(window, d, weights, cols, name):
+            weighted = keep.tile([P, cols.stop - cols.start], F32, name=name)
+            nc.vector.tensor_tensor(weighted[:], window[:].indirect(entries(pos_sb[d], cols)), weights[:, cols], MULT)
             return weighted
 
         ss = keep.tile([P, S], F32, name="ss")
-        ee_by_p0 = [neighbours(ee, 0, gate_sb[0], h, "ee_by_p0_%d" % h) for h in range(2)]
-        ee_by_p1 = [neighbours(ee, 1, gate_sb[1], h, "ee_by_p1_%d" % h) for h in range(2)]
+        ee_by_p0 = [neighbours_of(ee, 0, gate_sb[0], half[h], "ee_by_p0_%d" % h) for h in range(2)]
+        ee_by_p1 = [neighbours_of(ee, 1, gate_sb[1], half[h], "ee_by_p1_%d" % h) for h in range(2)]
         for h in range(2):
             nc.vector.tensor_tensor(ss[:, half[h]], ee_by_p0[h][:], ee_by_p1[h][:], ADD)
 
-        gate0_damped = keep.tile([P, S], F32, name="gate0_damped", tag="miss")
-        nc.scalar.activation(gate0_damped[:], gate_sb[0][:], COPY, scale=0.8)
+        routed = 4
+        gate0_turned = bank("back0", "gate0_turned")
+        for b in range(routed):
+            nc.tensor.transpose(gate0_turned[:, block[b]], gate_sb[0][:, block[b]], ident[:])
+        gate0_column = keep.tile([P, routed], F32, name="gate0_column")
+        nc.scalar.activation(gate0_column[:], gate0_turned[:, 0:routed * P:P], COPY, scale=0.4)
 
-        turned = [bank("turned%d" % b, "turned%d" % b) for b in range(BLOCKS)]
+        base_turned = keep.tile([P, S], F32, name="base_turned")
         for b in range(BLOCKS):
+            turned = bank("upright%d" % b, "base%d" % b)
             for i, term in enumerate((ee, p_sb, p_sb)):
-                nc.tensor.matmul(turned[b][:, 0:P], term[:, block[b]], ident[:], is_transpose=True,
-                                 start=(i == 0), stop=False)
+                nc.tensor.matmul(turned[:, 0:P], term[:, block[b]], ident[:], is_transpose=True,
+                                 start=(i == 0), stop=(i == 2))
+            nc.scalar.activation(base_turned[:, block[b]], turned[:, 0:P], COPY, scale=0.5)
+        back = [bank("back%d" % b, "back%d" % b) for b in range(BLOCKS)]
+        for b in range(BLOCKS):
+            nc.tensor.matmul(back[b][:, 0:P], base_turned[:, block[b]], ident[:], is_transpose=True,
+                             start=True, stop=(b >= routed))
 
-        ss_by_p0 = [neighbours(ss, 0, gate0_damped, h, "ss_by_p0_%d" % h) for h in range(2)]
-        ss_by_p1 = [neighbours(ss, 1, gate_sb[1], h, "ss_by_p1_%d" % h) for h in range(2)]
-        halved = keep.tile([P, S], F32, name="halved")
-        back = [bank("upright%d" % i, "back%d" % i) for i in range(3)]
-        partial = [back[0][:, block[0]], back[0][:, block[1]], back[1][:, 0:P], back[2][:, 0:P]]
-        for b in range(BLOCKS):
-            nc.tensor.matmul(turned[b][:, 0:P], ss_by_p0[b // 2][:, block[b % 2]], ident[:], is_transpose=True,
+        weighted_turned = keep.tile([P, routed * P], F32, name="weighted_turned")
+        for b in range(routed):
+            fetched = keep.tile([P, P], F32, name="ss_at_p0_%d" % b)
+            nc.vector.tensor_copy(fetched[:], ss[:].indirect(entries(pos_sb[0], block[b])))
+            turned = bank("upright%d" % b, "fetched%d" % b)
+            nc.tensor.transpose(turned[:, 0:P], fetched[:], ident[:])
+            nc.scalar.activation(weighted_turned[:, block[b]], turned[:, 0:P], COPY, scale=gate0_column[:, b:b + 1])
+            nc.tensor.matmul(back[b][:, 0:P], weighted_turned[:, block[b]], ident[:], is_transpose=True,
                              start=False, stop=True)
-            nc.scalar.activation(halved[:, block[b]], turned[b][:, 0:P], COPY, scale=0.5)
-        for b in range(BLOCKS):
-            nc.tensor.transpose(partial[b], halved[:, block[b]], ident[:])
+        rest = [back[b][:, 0:P] for b in range(BLOCKS)]
+        ss_by_p0 = [neighbours_of(ss, 0, gate_sb[0], block[b], "ss_by_p0_%d" % b) for b in range(routed, BLOCKS)]
+        ss_by_p1 = keep.tile([P, S], F32, name="ss_by_p1")
+        gathers = [[0,256],[256,512]]
+        for i, (first, last) in enumerate(gathers):
+            part = slice(first, last)
+            nc.vector.tensor_tensor(ss_by_p1[:, part], ss[:].indirect(entries(pos_sb[1], part)), gate_sb[1][:, part], MULT)
+            if i == 0:
+                for b in range(routed, BLOCKS):
+                    summed = keep.tile([P, P], F32, name="summed%d" % b)
+                    nc.vector.scalar_tensor_tensor(summed[:], ss_by_p0[b - routed][:], 0.4, rest[b], MULT, ADD)
+                    rest[b] = summed[:]
 
         result = keep.tile([P, S], F32, name="result")
-        nc.vector.scalar_tensor_tensor(result[:, half[0]], ss_by_p1[0][:], 0.4, back[0][:, 0:HALF], MULT, ADD)
-        nc.sync.dma_start(out=out[:, half[0]], in_=result[:, half[0]])
-        for b, queue in ((2, nc.scalar), (3, nc.sync)):
-            nc.vector.scalar_tensor_tensor(result[:, block[b]], ss_by_p1[1][:, block[b % 2]], 0.4, partial[b], MULT, ADD)
-            queue.dma_start(out=out[:, block[b]], in_=result[:, block[b]])
+        for blocks, queue in (((0, 1), nc.sync), ((2,), nc.scalar), ((3,), nc.sync)):
+            for b in blocks:
+                nc.vector.scalar_tensor_tensor(result[:, block[b]], ss_by_p1[:, block[b]], 0.4, rest[b], MULT, ADD)
+            part = slice(blocks[0] * P, (blocks[-1] + 1) * P)
+            queue.dma_start(out=out[:, part], in_=result[:, part])

@@ -34,36 +34,43 @@ def tile_picked_ycns_two_p_kernel(tc, x_words, x_scales, w1, gate, goal, known, 
         offs_sb = keep.tile([P, S // STRIPE], U16, name="offs_sb")
         pos_sb = [keep.tile([P, S // STRIPE], U16, name="pos%d_sb" % d) for d in range(2)]
         table_words = keep.tile([P, T], I32, name="table_words", align_bytes=64)
-        table_scales = keep.tile([P, T], U8, name="table_scales", align_bytes=64)
+        table_scales = keep.tile([P, T], U8, name="table_scales", tag="scales_slot", align_bytes=64)
         w_raw = keep.tile([P, PACK, N], F32, name="w_raw")
         goal_sb = keep.tile([P, S], F32, name="goal_sb")
-        known_sb = keep.tile([P, S], F32, name="known_sb")
-        gate_sb = [keep.tile([P, S], F32, name="gate%d_sb" % d) for d in range(2)]
 
         nc.vector.memset(table_scales[:].bitcast(I32), 0)
-        nc.sync.dma_start(out=w_raw[:], in_=w1.rearrange("(p j) m -> p j m", j=PACK))
+        nc.scalar.dma_start(out=w_raw[:], in_=w1.rearrange("(p j) m -> p j m", j=PACK))
         nc.sync.dma_start(offs_sb[:], offs)
-        for r in range(PACK):
-            queue = nc.sync if r < PACK // 2 else nc.scalar
-            queue.dma_start(out=table_scales[r:P:32, :].bitcast(I32), in_=x_scales[0, r:K // 32:PACK, :].bitcast(I32))
-        nc.sync.dma_start(out=table_words[:], in_=x_words[0].rearrange("p n t -> p (n t)").bitcast(I32))
-        nc.sync.dma_start(out=goal_sb[:], in_=goal)
-        nc.sync.dma_start(out=known_sb[:], in_=known)
         nc.sync.dma_start(pos_sb[0][:], pos1)
         nc.sync.dma_start(pos_sb[1][:], pos2)
-        for d in range(2):
-            nc.sync.dma_start(out=gate_sb[d][:], in_=gate[d])
+        rows = x_scales[0].bitcast(I32).rearrange("(e u r) c -> u r e c", e=2, u=2)
+        for u in range(2):
+            nc.sync.dma_start(out=table_scales[64 * u:64 * u + 8, :].bitcast(I32), in_=rows[u])
+        nc.sync.dma_start(out=table_words[:], in_=x_words[0].rearrange("p n t -> p (n t)").bitcast(I32))
+        nc.sync.dma_start(out=goal_sb[:], in_=goal)
         ident = keep.tile([P, P], F32, name="ident")
         make_identity(nc, ident[:])
 
-        w_grouped = keep.tile([P, N, PACK], BF16, name="w_grouped", align_bytes=64)
-        nc.vector.tensor_copy(out=w_grouped[:], in_=w_raw[:].rearrange("p j m -> p m j"))
         picked_scales = keep.tile([P, S], U8, name="picked_scales", align_bytes=64)
-        nc.vector.tensor_copy(picked_scales[:], table_scales[:].indirect(offs_sb[:]))
-        w_codes = keep.tile([P, N], U32, name="w_codes", align_bytes=64)
+        w_grouped = keep.tile([P, N, PACK], BF16, name="w_grouped", tag="grouped_slot", align_bytes=64)
+        nc.vector.tensor_copy(out=w_grouped[:], in_=w_raw[:].rearrange("p j m -> p m j"))
+        spread = keep.tile([P, S], U8, name="spread", align_bytes=64)
+        for h in range(2):
+            cols = slice(h * HALF, (h + 1) * HALF)
+            nc.vector.tensor_copy(spread[:, cols], table_scales[:].indirect(offs_sb[:, h * HALF // STRIPE:(h + 1) * HALF // STRIPE]))
+            for e in range(2):
+                nc.sync.dma_start(out=picked_scales[64 * e:64 * e + 64, cols].bitcast(I32), in_=spread[e:P:2, cols].bitcast(I32))
+
+        w_codes = keep.tile([P, N], U32, name="w_codes", tag="scales_slot", align_bytes=64)
         w_scales = keep.tile([P, N], U8, name="w_scales", align_bytes=64)
         nc.vector.quantize_mx(out=w_codes[:].bitcast(FP8X4), scales=w_scales[:],
                               in_=w_grouped[:].rearrange("p m j -> p (m j)"))
+        late = keep.tile([P, 3, S], F32, name="late", tag="grouped_slot", align_bytes=64)
+        known_sb = late[:, 0, :]
+        gate_sb = [late[:, 1, :], late[:, 2, :]]
+        nc.sync.dma_start(out=known_sb, in_=known)
+        for d in range(2):
+            nc.sync.dma_start(out=gate_sb[d], in_=gate[d])
 
         half = [slice(h * HALF, (h + 1) * HALF) for h in range(2)]
         block = [slice(b * P, (b + 1) * P) for b in range(BLOCKS)]
@@ -110,7 +117,7 @@ def tile_picked_ycns_two_p_kernel(tc, x_words, x_scales, w1, gate, goal, known, 
             nc.vector.tensor_tensor(ss[:, half[h]], ee_by_p0[h][:], ee_by_p1[h][:], ADD)
 
         routed = 4
-        gate0_turned = bank("back0", "gate0_turned")
+        gate0_turned = bank("upright0", "gate0_turned")
         for b in range(routed):
             nc.tensor.transpose(gate0_turned[:, block[b]], gate_sb[0][:, block[b]], ident[:])
         gate0_column = keep.tile([P, routed], F32, name="gate0_column")

@@ -38,22 +38,21 @@ def tile_picked_ycns_two_p_kernel(tc, x_words, x_scales, w1, gate, goal, known, 
         w_raw = keep.tile([P, PACK, N], F32, name="w_raw")
         goal_sb = keep.tile([P, S], F32, name="goal_sb")
 
-        nc.vector.memset(table_scales[:].bitcast(I32), 0)
-        nc.scalar.dma_start(out=w_raw[:], in_=w1.rearrange("(p j) m -> p j m", j=PACK))
+        rows = x_scales[0].bitcast(I32).rearrange("(e u r) c -> u r e c", e=2, u=2)
+        for u, queue in enumerate((nc.sync, nc.scalar)):
+            queue.dma_start(out=table_scales[64 * u + 24:64 * u + 32, :].bitcast(I32), in_=rows[u])
         nc.sync.dma_start(offs_sb[:], offs)
+        nc.scalar.dma_start(out=w_raw[:], in_=w1.rearrange("(p j) m -> p j m", j=PACK))
+        nc.sync.dma_start(out=table_words[:], in_=x_words[0].rearrange("p n t -> p (n t)").bitcast(I32))
         nc.sync.dma_start(pos_sb[0][:], pos1)
         nc.sync.dma_start(pos_sb[1][:], pos2)
-        rows = x_scales[0].bitcast(I32).rearrange("(e u r) c -> u r e c", e=2, u=2)
-        for u in range(2):
-            nc.sync.dma_start(out=table_scales[64 * u:64 * u + 8, :].bitcast(I32), in_=rows[u])
-        nc.sync.dma_start(out=table_words[:], in_=x_words[0].rearrange("p n t -> p (n t)").bitcast(I32))
         nc.sync.dma_start(out=goal_sb[:], in_=goal)
+        for first, last in ((0, 24), (32, 64), (64, 88), (96, 128)):
+            nc.vector.memset(table_scales[first:last, :].bitcast(I32), 0)
         ident = keep.tile([P, P], F32, name="ident")
         make_identity(nc, ident[:])
 
         picked_scales = keep.tile([P, S], U8, name="picked_scales", align_bytes=64)
-        w_grouped = keep.tile([P, N, PACK], BF16, name="w_grouped", tag="grouped_slot", align_bytes=64)
-        nc.vector.tensor_copy(out=w_grouped[:], in_=w_raw[:].rearrange("p j m -> p m j"))
         spread = keep.tile([P, S], U8, name="spread", align_bytes=64)
         for h in range(2):
             cols = slice(h * HALF, (h + 1) * HALF)
@@ -61,11 +60,13 @@ def tile_picked_ycns_two_p_kernel(tc, x_words, x_scales, w1, gate, goal, known, 
             for e in range(2):
                 nc.sync.dma_start(out=picked_scales[64 * e:64 * e + 64, cols].bitcast(I32), in_=spread[e:P:2, cols].bitcast(I32))
 
-        w_codes = keep.tile([P, N], U32, name="w_codes", tag="scales_slot", align_bytes=64)
+        w_grouped = keep.tile([P, N, PACK], BF16, name="w_grouped", tag="scales_slot", align_bytes=64)
+        nc.vector.tensor_copy(out=w_grouped[:], in_=w_raw[:].rearrange("p j m -> p m j"))
+        w_codes = keep.tile([P, N], U32, name="w_codes", align_bytes=64)
         w_scales = keep.tile([P, N], U8, name="w_scales", align_bytes=64)
         nc.vector.quantize_mx(out=w_codes[:].bitcast(FP8X4), scales=w_scales[:],
                               in_=w_grouped[:].rearrange("p m j -> p (m j)"))
-        late = keep.tile([P, 3, S], F32, name="late", tag="grouped_slot", align_bytes=64)
+        late = keep.tile([P, 3, S], F32, name="late", tag="scales_slot", align_bytes=64)
         known_sb = late[:, 0, :]
         gate_sb = [late[:, 1, :], late[:, 2, :]]
         nc.sync.dma_start(out=known_sb, in_=known)
@@ -96,7 +97,7 @@ def tile_picked_ycns_two_p_kernel(tc, x_words, x_scales, w1, gate, goal, known, 
             h = first // HALF
             nc.tensor.matmul_mx(out=logits[:, 0:last - first], lhsT=w_codes[:].bitcast(FP8X4), lhsT_scale=w_scales[:],
                                 rhs=picked_words[h][:, first - h * HALF:last - h * HALF].bitcast(FP8X4),
-                                rhs_scale=picked_scales[:, first:last], start=True, stop=True)
+                                rhs_scale=picked_scales[12:P, first:last], start=True, stop=True)
             nc.scalar.activation(p_sb[:, first:last], logits[:, 0:last - first], SIGMOID)
         for op, first, last in [[0,0,256],[1,0,256],[0,256,384],[1,256,384],[0,384,512],[1,384,512]]:
             part = slice(first, last)

@@ -39,10 +39,10 @@ def tile_picked_ycns_two_p_kernel(tc, x_words, x_scales, w1, gate, goal, known, 
         goal_sb = keep.tile([P, S], F32, name="goal_sb")
 
         rows = x_scales[0].bitcast(I32).rearrange("(e u r) c -> u r e c", e=2, u=2)
-        for u, queue in enumerate((nc.sync, nc.scalar)):
-            queue.dma_start(out=table_scales[64 * u + 24:64 * u + 32, :].bitcast(I32), in_=rows[u])
+        for u in range(2):
+            nc.scalar.dma_start(out=table_scales[64 * u + 24:64 * u + 32, :].bitcast(I32), in_=rows[u])
+        nc.sync.dma_start(out=w_raw[:], in_=w1.rearrange("(p j) m -> p j m", j=PACK))
         nc.sync.dma_start(offs_sb[:], offs)
-        nc.scalar.dma_start(out=w_raw[:], in_=w1.rearrange("(p j) m -> p j m", j=PACK))
         nc.sync.dma_start(out=table_words[:], in_=x_words[0].rearrange("p n t -> p (n t)").bitcast(I32))
         nc.sync.dma_start(pos_sb[0][:], pos1)
         nc.sync.dma_start(pos_sb[1][:], pos2)

@@ -39,16 +39,16 @@ def tile_picked_ycns_two_p_kernel(tc, x_words, x_scales, w1, gate, goal, known, 
         goal_sb = keep.tile([P, S], F32, name="goal_sb")
 
         rows = x_scales[0].bitcast(I32).rearrange("(e u r) c -> u r e c", e=2, u=2)
-        for u in range(2):
-            nc.scalar.dma_start(out=table_scales[64 * u + 24:64 * u + 32, :].bitcast(I32), in_=rows[u])
+        for first, last in ((0, 24), (32, 64), (64, 88), (96, 128)):
+            nc.vector.memset(table_scales[first:last, :].bitcast(I32), 0)
         nc.sync.dma_start(out=w_raw[:], in_=w1.rearrange("(p j) m -> p j m", j=PACK))
         nc.sync.dma_start(offs_sb[:], offs)
+        for u in range(2):
+            nc.sync.dma_start(out=table_scales[64 * u + 24:64 * u + 32, :].bitcast(I32), in_=rows[u])
         nc.sync.dma_start(out=table_words[:], in_=x_words[0].rearrange("p n t -> p (n t)").bitcast(I32))
         nc.sync.dma_start(pos_sb[0][:], pos1)
         nc.sync.dma_start(pos_sb[1][:], pos2)
         nc.sync.dma_start(out=goal_sb[:], in_=goal)
-        for first, last in ((0, 24), (32, 64), (64, 88), (96, 128)):
-            nc.vector.memset(table_scales[first:last, :].bitcast(I32), 0)
         ident = keep.tile([P, P], F32, name="ident")
         make_identity(nc, ident[:])
 

@@ -39,20 +39,23 @@ def tile_picked_ycns_two_p_kernel(tc, x_words, x_scales, w1, gate, goal, known, 
         goal_sb = keep.tile([P, S], F32, name="goal_sb")
 
         rows = x_scales[0].bitcast(I32).rearrange("(e u r) c -> u r e c", e=2, u=2)
-        for first, last in ((0, 24), (32, 64), (64, 88), (96, 128)):
-            nc.vector.memset(table_scales[first:last, :].bitcast(I32), 0)
+        for u in range(2):
+            nc.vector.memset(table_scales[64 * u:64 * u + 24, :].bitcast(I32), 0)
+            nc.gpsimd.memset(table_scales[64 * u + 32:64 * u + 64, :].bitcast(I32), 0)
         nc.sync.dma_start(out=w_raw[:], in_=w1.rearrange("(p j) m -> p j m", j=PACK))
         nc.sync.dma_start(offs_sb[:], offs)
         for u in range(2):
             nc.sync.dma_start(out=table_scales[64 * u + 24:64 * u + 32, :].bitcast(I32), in_=rows[u])
-        nc.sync.dma_start(out=table_words[:], in_=x_words[0].rearrange("p n t -> p (n t)").bitcast(I32))
         nc.sync.dma_start(pos_sb[0][:], pos1)
+        nc.sync.dma_start(out=table_words[:], in_=x_words[0].rearrange("p n t -> p (n t)").bitcast(I32))
         nc.sync.dma_start(pos_sb[1][:], pos2)
         nc.sync.dma_start(out=goal_sb[:], in_=goal)
         ident = keep.tile([P, P], F32, name="ident")
         make_identity(nc, ident[:])
 
         picked_scales = keep.tile([P, S], U8, name="picked_scales", align_bytes=64)
+        w_grouped = keep.tile([P, N, PACK], BF16, name="w_grouped", tag="grouped_slot", align_bytes=64)
+        nc.vector.tensor_copy(out=w_grouped[:], in_=w_raw[:].rearrange("p j m -> p m j"))
         spread = keep.tile([P, S], U8, name="spread", align_bytes=64)
         for h in range(2):
             cols = slice(h * HALF, (h + 1) * HALF)
@@ -60,13 +63,11 @@ def tile_picked_ycns_two_p_kernel(tc, x_words, x_scales, w1, gate, goal, known, 
             for e in range(2):
                 nc.sync.dma_start(out=picked_scales[64 * e:64 * e + 64, cols].bitcast(I32), in_=spread[e:P:2, cols].bitcast(I32))
 
-        w_grouped = keep.tile([P, N, PACK], BF16, name="w_grouped", tag="scales_slot", align_bytes=64)
-        nc.vector.tensor_copy(out=w_grouped[:], in_=w_raw[:].rearrange("p j m -> p m j"))
-        w_codes = keep.tile([P, N], U32, name="w_codes", align_bytes=64)
+        w_codes = keep.tile([P, N], U32, name="w_codes", tag="scales_slot", align_bytes=64)
         w_scales = keep.tile([P, N], U8, name="w_scales", align_bytes=64)
         nc.vector.quantize_mx(out=w_codes[:].bitcast(FP8X4), scales=w_scales[:],
                               in_=w_grouped[:].rearrange("p m j -> p (m j)"))
-        late = keep.tile([P, 3, S], F32, name="late", tag="scales_slot", align_bytes=64)
+        late = keep.tile([P, 3, S], F32, name="late", tag="grouped_slot", align_bytes=64)
         known_sb = late[:, 0, :]
         gate_sb = [late[:, 1, :], late[:, 2, :]]
         nc.sync.dma_start(out=known_sb, in_=known)
@@ -159,7 +160,7 @@ def tile_picked_ycns_two_p_kernel(tc, x_words, x_scales, w1, gate, goal, known, 
                     rest[b] = summed[:]
 
         result = keep.tile([P, S], F32, name="result")
-        for blocks, queue in (((0, 1), nc.sync), ((2,), nc.scalar), ((3,), nc.sync)):
+        for blocks, queue in (((0, 1), nc.sync), ((2,), nc.sync), ((3,), nc.sync)):
             for b in blocks:
                 nc.vector.scalar_tensor_tensor(result[:, block[b]], ss_by_p1[:, block[b]], 0.4, rest[b], MULT, ADD)
             part = slice(blocks[0] * P, (blocks[-1] + 1) * P)

@@ -42,12 +42,14 @@ def tile_picked_ycns_two_p_kernel(tc, x_words, x_scales, w1, gate, goal, known, 
         for u in range(2):
             nc.vector.memset(table_scales[64 * u:64 * u + 24, :].bitcast(I32), 0)
             nc.gpsimd.memset(table_scales[64 * u + 32:64 * u + 64, :].bitcast(I32), 0)
-        nc.sync.dma_start(out=w_raw[:], in_=w1.rearrange("(p j) m -> p j m", j=PACK))
-        nc.sync.dma_start(offs_sb[:], offs)
+        w_rows = w1.rearrange("(p j) m -> p j m", j=PACK)
+        nc.sync.dma_start(out=w_raw[:, 0:3, :], in_=w_rows[:, 0:3, :])
         for u in range(2):
             nc.sync.dma_start(out=table_scales[64 * u + 24:64 * u + 32, :].bitcast(I32), in_=rows[u])
-        nc.sync.dma_start(pos_sb[0][:], pos1)
+        nc.sync.dma_start(offs_sb[:], offs)
+        nc.sync.dma_start(out=w_raw[:, 3:4, :], in_=w_rows[:, 3:4, :])
         nc.sync.dma_start(out=table_words[:], in_=x_words[0].rearrange("p n t -> p (n t)").bitcast(I32))
+        nc.sync.dma_start(pos_sb[0][:], pos1)
         nc.sync.dma_start(pos_sb[1][:], pos2)
         nc.sync.dma_start(out=goal_sb[:], in_=goal)
         ident = keep.tile([P, P], F32, name="ident")

@@ -73,8 +73,7 @@ def tile_picked_ycns_two_p_kernel(tc, x_words, x_scales, w1, gate, goal, known, 
         known_sb = late[:, 0, :]
         gate_sb = [late[:, 1, :], late[:, 2, :]]
         nc.sync.dma_start(out=known_sb, in_=known)
-        for d in range(2):
-            nc.sync.dma_start(out=gate_sb[d], in_=gate[d])
+        nc.sync.dma_start(out=late[:, 1:3, :], in_=gate.rearrange("d p s -> p d s"))
 
         half = [slice(h * HALF, (h + 1) * HALF) for h in range(2)]
         block = [slice(b * P, (b + 1) * P) for b in range(BLOCKS)]
@@ -115,17 +114,26 @@ def tile_picked_ycns_two_p_kernel(tc, x_words, x_scales, w1, gate, goal, known, 
             return weighted
 
         ss = keep.tile([P, S], F32, name="ss")
-        ee_by_p0 = [neighbours_of(ee, 0, gate_sb[0], half[h], "ee_by_p0_%d" % h) for h in range(2)]
-        ee_by_p1 = [neighbours_of(ee, 1, gate_sb[1], half[h], "ee_by_p1_%d" % h) for h in range(2)]
-        for h in range(2):
-            nc.vector.tensor_tensor(ss[:, half[h]], ee_by_p0[h][:], ee_by_p1[h][:], ADD)
+        summed_turned = bank("back2", "summed_turned")
+        for d in range(2):
+            term = neighbours_of(ee, d, gate_sb[d], block[0], "ee_first_by_p%d" % d)
+            nc.tensor.matmul(summed_turned[:, 0:P], term[:], ident[:], is_transpose=True, start=(d == 0), stop=(d == 1))
+        first_turned = keep.tile([P, P], F32, name="first_turned")
+        nc.scalar.activation(first_turned[:], summed_turned[:, 0:P], COPY)
+        summed = bank("back3", "summed")
+        nc.tensor.transpose(summed[:, 0:P], first_turned[:], ident[:])
+        nc.scalar.activation(ss[:, block[0]], summed[:, 0:P], COPY)
+        ee_by_p0 = neighbours_of(ee, 0, gate_sb[0], slice(P, S), "ee_by_p0")
+        parts = (slice(P, S - P), block[3])
+        ee_by_p1 = [neighbours_of(ee, 1, gate_sb[1], part, "ee_by_p1_%d" % i) for i, part in enumerate(parts)]
+        for i, part in enumerate(parts):
+            nc.vector.tensor_tensor(ss[:, part], ee_by_p0[:, part.start - P:part.stop - P], ee_by_p1[i][:], ADD)
 
-        routed = 4
         gate0_turned = bank("upright0", "gate0_turned")
-        for b in range(routed):
+        for b in range(BLOCKS):
             nc.tensor.transpose(gate0_turned[:, block[b]], gate_sb[0][:, block[b]], ident[:])
-        gate0_column = keep.tile([P, routed], F32, name="gate0_column")
-        nc.scalar.activation(gate0_column[:], gate0_turned[:, 0:routed * P:P], COPY, scale=0.4)
+        gate0_column = keep.tile([P, BLOCKS], F32, name="gate0_column")
+        nc.scalar.activation(gate0_column[:], gate0_turned[:, 0:S:P], COPY, scale=0.4)
 
         base_turned = keep.tile([P, S], F32, name="base_turned")
         for b in range(BLOCKS):
@@ -134,36 +142,27 @@ def tile_picked_ycns_two_p_kernel(tc, x_words, x_scales, w1, gate, goal, known, 
                 nc.tensor.matmul(turned[:, 0:P], term[:, block[b]], ident[:], is_transpose=True,
                                  start=(i == 0), stop=(i == 2))
             nc.scalar.activation(base_turned[:, block[b]], turned[:, 0:P], COPY, scale=0.5)
-        back = [bank("back%d" % b, "back%d" % b) for b in range(BLOCKS)]
+        pieces = (half[0], block[2], block[3])
+        back = [bank("back%d" % (i + 1), "back%d" % i) for i in range(len(pieces))]
+        piece_of = (0, 0, 1, 2)
         for b in range(BLOCKS):
-            nc.tensor.matmul(back[b][:, 0:P], base_turned[:, block[b]], ident[:], is_transpose=True,
-                             start=True, stop=(b >= routed))
+            nc.tensor.matmul(back[piece_of[b]][:, block[b]], base_turned[:, block[b]], ident[:], is_transpose=True,
+                             start=(b != 1), stop=False)
 
-        weighted_turned = keep.tile([P, routed * P], F32, name="weighted_turned")
-        for b in range(routed):
+        weighted_turned = keep.tile([P, S], F32, name="weighted_turned")
+        for b in range(BLOCKS):
             fetched = keep.tile([P, P], F32, name="ss_at_p0_%d" % b)
             nc.vector.tensor_copy(fetched[:], ss[:].indirect(entries(pos_sb[0], block[b])))
             turned = bank("upright%d" % b, "fetched%d" % b)
             nc.tensor.transpose(turned[:, 0:P], fetched[:], ident[:])
             nc.scalar.activation(weighted_turned[:, block[b]], turned[:, 0:P], COPY, scale=gate0_column[:, b:b + 1])
-            nc.tensor.matmul(back[b][:, 0:P], weighted_turned[:, block[b]], ident[:], is_transpose=True,
-                             start=False, stop=True)
-        rest = [back[b][:, 0:P] for b in range(BLOCKS)]
-        ss_by_p0 = [neighbours_of(ss, 0, gate_sb[0], block[b], "ss_by_p0_%d" % b) for b in range(routed, BLOCKS)]
+            nc.tensor.matmul(back[piece_of[b]][:, block[b]], weighted_turned[:, block[b]], ident[:], is_transpose=True,
+                             start=False, stop=(b != 0))
         ss_by_p1 = keep.tile([P, S], F32, name="ss_by_p1")
-        gathers = [[0,256],[256,512]]
-        for i, (first, last) in enumerate(gathers):
-            part = slice(first, last)
+        for part in half:
             nc.vector.tensor_tensor(ss_by_p1[:, part], ss[:].indirect(entries(pos_sb[1], part)), gate_sb[1][:, part], MULT)
-            if i == 0:
-                for b in range(routed, BLOCKS):
-                    summed = keep.tile([P, P], F32, name="summed%d" % b)
-                    nc.vector.scalar_tensor_tensor(summed[:], ss_by_p0[b - routed][:], 0.4, rest[b], MULT, ADD)
-                    rest[b] = summed[:]
 
         result = keep.tile([P, S], F32, name="result")
-        for blocks, queue in (((0, 1), nc.sync), ((2,), nc.sync), ((3,), nc.sync)):
-            for b in blocks:
-                nc.vector.scalar_tensor_tensor(result[:, block[b]], ss_by_p1[:, block[b]], 0.4, rest[b], MULT, ADD)
-            part = slice(blocks[0] * P, (blocks[-1] + 1) * P)
-            queue.dma_start(out=out[:, part], in_=result[:, part])
+        for i, part in enumerate(pieces):
+            nc.vector.scalar_tensor_tensor(result[:, part], ss_by_p1[:, part], 0.4, back[i][:, part], MULT, ADD)
+            nc.sync.dma_start(out=out[:, part], in_=result[:, part])

@@ -73,7 +73,8 @@ def tile_picked_ycns_two_p_kernel(tc, x_words, x_scales, w1, gate, goal, known, 
         known_sb = late[:, 0, :]
         gate_sb = [late[:, 1, :], late[:, 2, :]]
         nc.sync.dma_start(out=known_sb, in_=known)
-        nc.sync.dma_start(out=late[:, 1:3, :], in_=gate.rearrange("d p s -> p d s"))
+        for cols in (slice(0, P), slice(P, S)):
+            nc.sync.dma_start(out=late[:, 1:3, cols], in_=gate[:, :, cols].rearrange("d p s -> p d s"))
 
         half = [slice(h * HALF, (h + 1) * HALF) for h in range(2)]
         block = [slice(b * P, (b + 1) * P) for b in range(BLOCKS)]
@@ -136,12 +137,13 @@ def tile_picked_ycns_two_p_kernel(tc, x_words, x_scales, w1, gate, goal, known, 
         nc.scalar.activation(gate0_column[:], gate0_turned[:, 0:S:P], COPY, scale=0.4)
 
         base_turned = keep.tile([P, S], F32, name="base_turned")
-        for b in range(BLOCKS):
-            turned = bank("upright%d" % b, "base%d" % b)
-            for i, term in enumerate((ee, p_sb, p_sb)):
-                nc.tensor.matmul(turned[:, 0:P], term[:, block[b]], ident[:], is_transpose=True,
-                                 start=(i == 0), stop=(i == 2))
-            nc.scalar.activation(base_turned[:, block[b]], turned[:, 0:P], COPY, scale=0.5)
+        for h in range(2):
+            turned = bank("upright%d" % h, "base%d" % h)
+            for b in (2 * h, 2 * h + 1):
+                for i, term in enumerate((ee, p_sb, p_sb)):
+                    nc.tensor.matmul(turned[:, block[b]], term[:, block[b]], ident[:], is_transpose=True,
+                                     start=(i == 0), stop=(i == 2))
+            nc.scalar.activation(base_turned[:, half[h]], turned[:, half[h]], COPY, scale=0.5)
         pieces = (half[0], block[2], block[3])
         back = [bank("back%d" % (i + 1), "back%d" % i) for i in range(len(pieces))]
         piece_of = (0, 0, 1, 2)
@@ -153,9 +155,10 @@ def tile_picked_ycns_two_p_kernel(tc, x_words, x_scales, w1, gate, goal, known, 
         for b in range(BLOCKS):
             fetched = keep.tile([P, P], F32, name="ss_at_p0_%d" % b)
             nc.vector.tensor_copy(fetched[:], ss[:].indirect(entries(pos_sb[0], block[b])))
-            turned = bank("upright%d" % b, "fetched%d" % b)
+            turned = bank(("upright2", "upright3", "back0", "upright0")[b], "fetched%d" % b)
             nc.tensor.transpose(turned[:, 0:P], fetched[:], ident[:])
             nc.scalar.activation(weighted_turned[:, block[b]], turned[:, 0:P], COPY, scale=gate0_column[:, b:b + 1])
+        for b in range(BLOCKS):
             nc.tensor.matmul(back[piece_of[b]][:, block[b]], weighted_turned[:, block[b]], ident[:], is_transpose=True,
                              start=False, stop=(b != 0))
         ss_by_p1 = keep.tile([P, S], F32, name="ss_by_p1")

@@ -138,11 +138,11 @@ def tile_picked_ycns_two_p_kernel(tc, x_words, x_scales, w1, gate, goal, known, 
 
         base_turned = keep.tile([P, S], F32, name="base_turned")
         for h in range(2):
-            turned = bank("upright%d" % h, "base%d" % h)
-            for b in (2 * h, 2 * h + 1):
-                for i, term in enumerate((ee, p_sb, p_sb)):
-                    nc.tensor.matmul(turned[:, block[b]], term[:, block[b]], ident[:], is_transpose=True,
-                                     start=(i == 0), stop=(i == 2))
+            turned = bank("upright%d" % (2 + h), "base%d" % h)
+            terms = [(term, b) for term in (p_sb, p_sb, ee) for b in (2 * h, 2 * h + 1)]
+            for i, (term, b) in enumerate(terms):
+                nc.tensor.matmul(turned[:, block[b]], term[:, block[b]], ident[:], is_transpose=True,
+                                 start=(i == 0), stop=(i == len(terms) - 1))
             nc.scalar.activation(base_turned[:, half[h]], turned[:, half[h]], COPY, scale=0.5)
         pieces = (half[0], block[2], block[3])
         back = [bank("back%d" % (i + 1), "back%d" % i) for i in range(len(pieces))]
@@ -155,7 +155,7 @@ def tile_picked_ycns_two_p_kernel(tc, x_words, x_scales, w1, gate, goal, known, 
         for b in range(BLOCKS):
             fetched = keep.tile([P, P], F32, name="ss_at_p0_%d" % b)
             nc.vector.tensor_copy(fetched[:], ss[:].indirect(entries(pos_sb[0], block[b])))
-            turned = bank(("upright2", "upright3", "back0", "upright0")[b], "fetched%d" % b)
+            turned = bank(("upright1", "back0", "upright0", "upright2")[b], "fetched%d" % b)
             nc.tensor.transpose(turned[:, 0:P], fetched[:], ident[:])
             nc.scalar.activation(weighted_turned[:, block[b]], turned[:, 0:P], COPY, scale=gate0_column[:, b:b + 1])
         for b in range(BLOCKS):

@@ -130,12 +130,6 @@ def tile_picked_ycns_two_p_kernel(tc, x_words, x_scales, w1, gate, goal, known, 
         for i, part in enumerate(parts):
             nc.vector.tensor_tensor(ss[:, part], ee_by_p0[:, part.start - P:part.stop - P], ee_by_p1[i][:], ADD)
 
-        gate0_turned = bank("upright0", "gate0_turned")
-        for b in range(BLOCKS):
-            nc.tensor.transpose(gate0_turned[:, block[b]], gate_sb[0][:, block[b]], ident[:])
-        gate0_column = keep.tile([P, BLOCKS], F32, name="gate0_column")
-        nc.scalar.activation(gate0_column[:], gate0_turned[:, 0:S:P], COPY, scale=0.4)
-
         base_turned = keep.tile([P, S], F32, name="base_turned")
         for h in range(2):
             turned = bank("upright%d" % (2 + h), "base%d" % h)
@@ -153,11 +147,10 @@ def tile_picked_ycns_two_p_kernel(tc, x_words, x_scales, w1, gate, goal, known, 
 
         weighted_turned = keep.tile([P, S], F32, name="weighted_turned")
         for b in range(BLOCKS):
-            fetched = keep.tile([P, P], F32, name="ss_at_p0_%d" % b)
-            nc.vector.tensor_copy(fetched[:], ss[:].indirect(entries(pos_sb[0], block[b])))
+            fetched = neighbours_of(ss, 0, gate_sb[0], block[b], "ss_by_p0_%d" % b)
             turned = bank(("upright1", "back0", "upright0", "upright2")[b], "fetched%d" % b)
             nc.tensor.transpose(turned[:, 0:P], fetched[:], ident[:])
-            nc.scalar.activation(weighted_turned[:, block[b]], turned[:, 0:P], COPY, scale=gate0_column[:, b:b + 1])
+            nc.scalar.activation(weighted_turned[:, block[b]], turned[:, 0:P], COPY, scale=0.4)
         for b in range(BLOCKS):
             nc.tensor.matmul(back[piece_of[b]][:, block[b]], weighted_turned[:, block[b]], ident[:], is_transpose=True,
                              start=False, stop=(b != 0))

@@ -73,8 +73,8 @@ def tile_picked_ycns_two_p_kernel(tc, x_words, x_scales, w1, gate, goal, known, 
         known_sb = late[:, 0, :]
         gate_sb = [late[:, 1, :], late[:, 2, :]]
         nc.sync.dma_start(out=known_sb, in_=known)
-        for cols in (slice(0, P), slice(P, S)):
-            nc.sync.dma_start(out=late[:, 1:3, cols], in_=gate[:, :, cols].rearrange("d p s -> p d s"))
+        for d in range(2):
+            nc.sync.dma_start(out=gate_sb[d], in_=gate[d])
 
         half = [slice(h * HALF, (h + 1) * HALF) for h in range(2)]
         block = [slice(b * P, (b + 1) * P) for b in range(BLOCKS)]
@@ -115,20 +115,9 @@ def tile_picked_ycns_two_p_kernel(tc, x_words, x_scales, w1, gate, goal, known, 
             return weighted
 
         ss = keep.tile([P, S], F32, name="ss")
-        summed_turned = bank("back2", "summed_turned")
-        for d in range(2):
-            term = neighbours_of(ee, d, gate_sb[d], block[0], "ee_first_by_p%d" % d)
-            nc.tensor.matmul(summed_turned[:, 0:P], term[:], ident[:], is_transpose=True, start=(d == 0), stop=(d == 1))
-        first_turned = keep.tile([P, P], F32, name="first_turned")
-        nc.scalar.activation(first_turned[:], summed_turned[:, 0:P], COPY)
-        summed = bank("back3", "summed")
-        nc.tensor.transpose(summed[:, 0:P], first_turned[:], ident[:])
-        nc.scalar.activation(ss[:, block[0]], summed[:, 0:P], COPY)
-        ee_by_p0 = neighbours_of(ee, 0, gate_sb[0], slice(P, S), "ee_by_p0")
-        parts = (slice(P, S - P), block[3])
-        ee_by_p1 = [neighbours_of(ee, 1, gate_sb[1], part, "ee_by_p1_%d" % i) for i, part in enumerate(parts)]
-        for i, part in enumerate(parts):
-            nc.vector.tensor_tensor(ss[:, part], ee_by_p0[:, part.start - P:part.stop - P], ee_by_p1[i][:], ADD)
+        ee_by = [[neighbours_of(ee, d, gate_sb[d], half[h], "ee_by_p%d_%d" % (d, h)) for h in range(2)] for d in range(2)]
+        for h in range(2):
+            nc.vector.tensor_tensor(ss[:, half[h]], ee_by[0][h][:], ee_by[1][h][:], ADD)
 
         base_turned = keep.tile([P, S], F32, name="base_turned")
         for h in range(2):
@@ -151,7 +140,6 @@ def tile_picked_ycns_two_p_kernel(tc, x_words, x_scales, w1, gate, goal, known, 
             turned = bank(("upright1", "back0", "upright0", "upright2")[b], "fetched%d" % b)
             nc.tensor.transpose(turned[:, 0:P], fetched[:], ident[:])
             nc.scalar.activation(weighted_turned[:, block[b]], turned[:, 0:P], COPY, scale=0.4)
-        for b in range(BLOCKS):
             nc.tensor.matmul(back[piece_of[b]][:, block[b]], weighted_turned[:, block[b]], ident[:], is_transpose=True,
                              start=False, stop=(b != 0))
         ss_by_p1 = keep.tile([P, S], F32, name="ss_by_p1")

@@ -87,7 +87,8 @@ def tile_picked_ycns_two_p_kernel(tc, x_words, x_scales, w1, gate, goal, known, 
 
         p_sb = keep.tile([P, S], F32, name="p_sb")
         miss = keep.tile([P, S], F32, name="miss")
-        ee = keep.tile([P, S], F32, name="ee")
+        ee = keep.tile([P, S + STRIPE], F32, name="ee")
+        nc.vector.memset(ee[:, S:S + STRIPE], 0.0)
         picked_words = []
         for h in range(2):
             words = keep.tile([P, HALF], U32, name="picked_words%d" % h, align_bytes=64)
@@ -115,9 +116,10 @@ def tile_picked_ycns_two_p_kernel(tc, x_words, x_scales, w1, gate, goal, known, 
             return weighted
 
         ss = keep.tile([P, S], F32, name="ss")
-        ee_by = [[neighbours_of(ee, d, gate_sb[d], half[h], "ee_by_p%d_%d" % (d, h)) for h in range(2)] for d in range(2)]
+        ee_by_p0 = neighbours_of(ee, 0, gate_sb[0], slice(0, S), "ee_by_p0")
+        ee_by_p1 = [neighbours_of(ee, 1, gate_sb[1], half[h], "ee_by_p1_%d" % h) for h in range(2)]
         for h in range(2):
-            nc.vector.tensor_tensor(ss[:, half[h]], ee_by[0][h][:], ee_by[1][h][:], ADD)
+            nc.vector.tensor_tensor(ss[:, half[h]], ee_by_p0[:, half[h]], ee_by_p1[h][:], ADD)
 
         base_turned = keep.tile([P, S], F32, name="base_turned")
         for h in range(2):

@@ -20,8 +20,7 @@ U8 = mybir.dt.uint8
 FP8X4 = mybir.dt.float8_e4m3fn_x4
 MULT = mybir.AluOpType.mult
 ADD = mybir.AluOpType.add
-SUB = mybir.AluOpType.subtract
-SIGMOID = mybir.ActivationFunctionType.Sigmoid
+TANH = mybir.ActivationFunctionType.Tanh
 COPY = mybir.ActivationFunctionType.Copy
 
 
@@ -73,7 +72,7 @@ def tile_picked_ycns_two_p_kernel(tc, x_words, x_scales, w1, gate, goal, known, 
         known_sb = late[:, 0, :]
         gate_sb = [late[:, 1, :], late[:, 2, :]]
         nc.sync.dma_start(out=known_sb, in_=known)
-        for d in range(2):
+        for d in (1, 0):
             nc.sync.dma_start(out=gate_sb[d], in_=gate[d])
 
         half = [slice(h * HALF, (h + 1) * HALF) for h in range(2)]
@@ -102,53 +101,72 @@ def tile_picked_ycns_two_p_kernel(tc, x_words, x_scales, w1, gate, goal, known, 
             nc.tensor.matmul_mx(out=logits[:, 0:last - first], lhsT=w_codes[:].bitcast(FP8X4), lhsT_scale=w_scales[:],
                                 rhs=picked_words[h][:, first - h * HALF:last - h * HALF].bitcast(FP8X4),
                                 rhs_scale=picked_scales[12:P, first:last], start=True, stop=True)
-            nc.scalar.activation(p_sb[:, first:last], logits[:, 0:last - first], SIGMOID)
+            nc.scalar.activation(p_sb[:, first:last], logits[:, 0:last - first], TANH, scale=0.5)
         for op, first, last in [[0,0,256],[1,0,256],[0,256,384],[1,256,384],[0,384,512],[1,384,512]]:
             part = slice(first, last)
             if op == 0:
-                nc.vector.tensor_tensor(miss[:, part], goal_sb[:, part], p_sb[:, part], SUB)
+                nc.vector.scalar_tensor_tensor(miss[:, part], p_sb[:, part], -0.5, goal_sb[:, part], MULT, ADD)
             else:
-                nc.vector.tensor_tensor(ee[:, part], miss[:, part], known_sb[:, part], MULT)
+                nc.vector.scalar_tensor_tensor(ee[:, part], miss[:, part], -0.5, known_sb[:, part], ADD, MULT)
 
-        def neighbours_of(window, d, weights, cols, name):
-            weighted = keep.tile([P, cols.stop - cols.start], F32, name=name)
-            nc.vector.tensor_tensor(weighted[:], window[:].indirect(entries(pos_sb[d], cols)), weights[:, cols], MULT)
-            return weighted
+        def fetch(window, d, cols, into):
+            nc.scalar.activation(into, window[:].indirect(entries(pos_sb[d], cols)), COPY)
+
+        def fetch_weighted(window, d, cols, into):
+            nc.vector.tensor_tensor(into, window[:].indirect(entries(pos_sb[d], cols)), gate_sb[d][:, cols], MULT)
 
         ss = keep.tile([P, S], F32, name="ss")
-        ee_by_p0 = neighbours_of(ee, 0, gate_sb[0], slice(0, S), "ee_by_p0")
-        ee_by_p1 = [neighbours_of(ee, 1, gate_sb[1], half[h], "ee_by_p1_%d" % h) for h in range(2)]
+        second = keep.tile([P, S], F32, name="second")
+        fetch_weighted(ee, 1, slice(0, S), second[:])
+        first = [keep.tile([P, HALF], F32, name="first%d" % h, tag="first_slot%d" % h) for h in range(2)]
+        first_w = keep.tile([P, S], F32, name="first_w")
         for h in range(2):
-            nc.vector.tensor_tensor(ss[:, half[h]], ee_by_p0[:, half[h]], ee_by_p1[h][:], ADD)
+            fetch(ee, 0, half[h], first[h][:])
+        for h in range(2):
+            nc.vector.tensor_tensor(first_w[:, half[h]], first[h][:], gate_sb[0][:, half[h]], MULT)
+        for h in range(2):
+            nc.vector.tensor_tensor(ss[:, half[h]], first_w[:, half[h]], second[:, half[h]], ADD)
 
-        base_turned = keep.tile([P, S], F32, name="base_turned")
+        base_turned = keep.tile([P, S], F32, name="base_turned", tag="first_slot0")
         for h in range(2):
             turned = bank("upright%d" % (2 + h), "base%d" % h)
-            terms = [(term, b) for term in (p_sb, p_sb, ee) for b in (2 * h, 2 * h + 1)]
+            terms = [(term, b) for term in (p_sb, ee) for b in (2 * h, 2 * h + 1)]
             for i, (term, b) in enumerate(terms):
                 nc.tensor.matmul(turned[:, block[b]], term[:, block[b]], ident[:], is_transpose=True,
                                  start=(i == 0), stop=(i == len(terms) - 1))
-            nc.scalar.activation(base_turned[:, half[h]], turned[:, half[h]], COPY, scale=0.5)
-        pieces = (half[0], block[2], block[3])
-        back = [bank("back%d" % (i + 1), "back%d" % i) for i in range(len(pieces))]
-        piece_of = (0, 0, 1, 2)
+            nc.scalar.activation(base_turned[:, half[h]], turned[:, half[h]], COPY, scale=0.5, bias=0.5)
+        gate_turned = bank("upright2", "gate_turned")
+        for b in range(2):
+            nc.tensor.transpose(gate_turned[:, block[b]], gate_sb[0][:, block[b]], ident[:])
+        gate_column = keep.tile([P, 2], F32, name="gate_column")
+        nc.scalar.activation(gate_column[:], gate_turned[:, 0:HALF:P], COPY, scale=0.4)
+        back = [bank("back%d" % (h + 1), "back%d" % h) for h in range(2)]
         for b in range(BLOCKS):
-            nc.tensor.matmul(back[piece_of[b]][:, block[b]], base_turned[:, block[b]], ident[:], is_transpose=True,
-                             start=(b != 1), stop=False)
+            nc.tensor.matmul(back[b // 2][:, block[b]], base_turned[:, block[b]], ident[:], is_transpose=True,
+                             start=(b % 2 == 0), stop=(b == 3))
 
-        weighted_turned = keep.tile([P, S], F32, name="weighted_turned")
-        for b in range(BLOCKS):
-            fetched = neighbours_of(ss, 0, gate_sb[0], block[b], "ss_by_p0_%d" % b)
-            turned = bank(("upright1", "back0", "upright0", "upright2")[b], "fetched%d" % b)
-            nc.tensor.transpose(turned[:, 0:P], fetched[:], ident[:])
-            nc.scalar.activation(weighted_turned[:, block[b]], turned[:, 0:P], COPY, scale=0.4)
-            nc.tensor.matmul(back[piece_of[b]][:, block[b]], weighted_turned[:, block[b]], ident[:], is_transpose=True,
-                             start=False, stop=(b != 0))
+        weighted_turned = keep.tile([P, HALF], F32, name="weighted_turned")
+        fetched = [keep.tile([P, P], F32, name="fetched%d" % b) for b in range(2)]
+        for b in range(2):
+            fetch(ss, 0, block[b], fetched[b][:])
+        fetched_upper = keep.tile([P, HALF], F32, name="fetched_upper")
+        fetch(ss, 0, half[1], fetched_upper[:])
         ss_by_p1 = keep.tile([P, S], F32, name="ss_by_p1")
-        for part in half:
-            nc.vector.tensor_tensor(ss_by_p1[:, part], ss[:].indirect(entries(pos_sb[1], part)), gate_sb[1][:, part], MULT)
+        for h in (1, 0):
+            fetch_weighted(ss, 1, half[h], ss_by_p1[:, half[h]])
+        for b in range(2):
+            turned = bank(("upright1", "back0")[b], "fetched_turned%d" % b)
+            nc.tensor.transpose(turned[:, 0:P], fetched[b][:], ident[:])
+            nc.scalar.activation(weighted_turned[:, block[b]], turned[:, 0:P], COPY, scale=gate_column[:, b:b + 1])
+            nc.tensor.matmul(back[0][:, block[b]], weighted_turned[:, block[b]], ident[:], is_transpose=True,
+                             start=False, stop=(b == 1))
 
         result = keep.tile([P, S], F32, name="result")
-        for i, part in enumerate(pieces):
-            nc.vector.scalar_tensor_tensor(result[:, part], ss_by_p1[:, part], 0.4, back[i][:, part], MULT, ADD)
-            nc.sync.dma_start(out=out[:, part], in_=result[:, part])
+        partial = keep.tile([P, HALF], F32, name="partial")
+        upper_w = keep.tile([P, HALF], F32, name="upper_w")
+        nc.vector.scalar_tensor_tensor(partial[:], ss_by_p1[:, half[1]], 0.4, back[1][:, half[1]], MULT, ADD)
+        nc.vector.tensor_tensor(upper_w[:], fetched_upper[:], gate_sb[0][:, half[1]], MULT)
+        nc.vector.scalar_tensor_tensor(result[:, half[1]], upper_w[:], 0.4, partial[:], MULT, ADD)
+        nc.sync.dma_start(out=out[:, half[1]], in_=result[:, half[1]])
+        nc.vector.scalar_tensor_tensor(result[:, half[0]], ss_by_p1[:, half[0]], 0.4, back[0][:, half[0]], MULT, ADD)
+        nc.sync.dma_start(out=out[:, half[0]], in_=result[:, half[0]])

@@ -46,9 +46,9 @@ def tile_picked_ycns_two_p_kernel(tc, x_words, x_scales, w1, gate, goal, known, 
         for u in range(2):
             nc.sync.dma_start(out=table_scales[64 * u + 24:64 * u + 32, :].bitcast(I32), in_=rows[u])
         nc.sync.dma_start(offs_sb[:], offs)
+        nc.sync.dma_start(pos_sb[0][:], pos1)
         nc.sync.dma_start(out=w_raw[:, 3:4, :], in_=w_rows[:, 3:4, :])
         nc.sync.dma_start(out=table_words[:], in_=x_words[0].rearrange("p n t -> p (n t)").bitcast(I32))
-        nc.sync.dma_start(pos_sb[0][:], pos1)
         nc.sync.dma_start(pos_sb[1][:], pos2)
         nc.sync.dma_start(out=goal_sb[:], in_=goal)
         ident = keep.tile([P, P], F32, name="ident")
@@ -88,26 +88,19 @@ def tile_picked_ycns_two_p_kernel(tc, x_words, x_scales, w1, gate, goal, known, 
         miss = keep.tile([P, S], F32, name="miss")
         ee = keep.tile([P, S + STRIPE], F32, name="ee")
         nc.vector.memset(ee[:, S:S + STRIPE], 0.0)
-        picked_words = []
-        for h in range(2):
-            words = keep.tile([P, HALF], U32, name="picked_words%d" % h, align_bytes=64)
-            nc.vector.tensor_copy(words[:], table_words[:].bitcast(U32).indirect(entries(offs_sb, half[h])))
-            picked_words.append(words)
-        products = [[0,128],[128,256],[256,384],[384,512]]
-        tags = ["upright0", "upright1", "upright2", "upright3", "back3", "back2"]
-        for i, (first, last) in enumerate(products):
-            logits = bank(tags[i], "logits%d" % i)
-            h = first // HALF
-            nc.tensor.matmul_mx(out=logits[:, 0:last - first], lhsT=w_codes[:].bitcast(FP8X4), lhsT_scale=w_scales[:],
-                                rhs=picked_words[h][:, first - h * HALF:last - h * HALF].bitcast(FP8X4),
-                                rhs_scale=picked_scales[12:P, first:last], start=True, stop=True)
-            nc.scalar.activation(p_sb[:, first:last], logits[:, 0:last - first], TANH, scale=0.5)
-        for op, first, last in [[0,0,256],[1,0,256],[0,256,384],[1,256,384],[0,384,512],[1,384,512]]:
-            part = slice(first, last)
-            if op == 0:
-                nc.vector.scalar_tensor_tensor(miss[:, part], p_sb[:, part], -0.5, goal_sb[:, part], MULT, ADD)
-            else:
-                nc.vector.scalar_tensor_tensor(ee[:, part], miss[:, part], -0.5, known_sb[:, part], ADD, MULT)
+        for part in (half[0], block[2], block[3]):
+            words = keep.tile([P, part.stop - part.start], U32, name="picked_words%d" % part.start, align_bytes=64)
+            nc.vector.tensor_copy(words[:], table_words[:].bitcast(U32).indirect(entries(offs_sb, part)))
+            for b in range(part.start // P, part.stop // P):
+                logits = bank("upright%d" % b, "logits%d" % b)
+                nc.tensor.matmul_mx(out=logits[:, 0:P], lhsT=w_codes[:].bitcast(FP8X4), lhsT_scale=w_scales[:],
+                                    rhs=words[:, b * P - part.start:(b + 1) * P - part.start].bitcast(FP8X4),
+                                    rhs_scale=picked_scales[12:P, block[b]], start=True, stop=True)
+                nc.scalar.activation(p_sb[:, block[b]], logits[:, 0:P], TANH, scale=0.5)
+        for part in (half[0], block[2], block[3]):
+            nc.vector.scalar_tensor_tensor(miss[:, part], p_sb[:, part], -0.5, goal_sb[:, part], MULT, ADD)
+        for part in half:
+            nc.vector.scalar_tensor_tensor(ee[:, part], miss[:, part], -0.5, known_sb[:, part], ADD, MULT)
 
         def fetch(window, d, cols, into):
             nc.scalar.activation(into, window[:].indirect(entries(pos_sb[d], cols)), COPY)
@@ -140,33 +133,35 @@ def tile_picked_ycns_two_p_kernel(tc, x_words, x_scales, w1, gate, goal, known, 
             nc.tensor.transpose(gate_turned[:, block[b]], gate_sb[0][:, block[b]], ident[:])
         gate_column = keep.tile([P, 2], F32, name="gate_column")
         nc.scalar.activation(gate_column[:], gate_turned[:, 0:HALF:P], COPY, scale=0.4)
-        back = [bank("back%d" % (h + 1), "back%d" % h) for h in range(2)]
+        back = [bank("back%d" % (i + 1), "back%d" % i) for i in range(3)]
         for b in range(BLOCKS):
-            nc.tensor.matmul(back[b // 2][:, block[b]], base_turned[:, block[b]], ident[:], is_transpose=True,
-                             start=(b % 2 == 0), stop=(b == 3))
+            nc.tensor.matmul(back[min(b, 2)][:, block[b]], base_turned[:, block[b]], ident[:], is_transpose=True,
+                             start=(b != 3), stop=(b == 3))
 
         weighted_turned = keep.tile([P, HALF], F32, name="weighted_turned")
-        fetched = [keep.tile([P, P], F32, name="fetched%d" % b) for b in range(2)]
+        fetched = [keep.tile([P, HALF], F32, name="fetched%d" % h) for h in range(2)]
         for b in range(2):
-            fetch(ss, 0, block[b], fetched[b][:])
-        fetched_upper = keep.tile([P, HALF], F32, name="fetched_upper")
-        fetch(ss, 0, half[1], fetched_upper[:])
+            fetch(ss, 0, block[b], fetched[0][:, block[b]])
+        fetch(ss, 0, half[1], fetched[1][:])
         ss_by_p1 = keep.tile([P, S], F32, name="ss_by_p1")
         for h in (1, 0):
             fetch_weighted(ss, 1, half[h], ss_by_p1[:, half[h]])
         for b in range(2):
             turned = bank(("upright1", "back0")[b], "fetched_turned%d" % b)
-            nc.tensor.transpose(turned[:, 0:P], fetched[b][:], ident[:])
+            nc.tensor.transpose(turned[:, 0:P], fetched[0][:, block[b]], ident[:])
             nc.scalar.activation(weighted_turned[:, block[b]], turned[:, 0:P], COPY, scale=gate_column[:, b:b + 1])
-            nc.tensor.matmul(back[0][:, block[b]], weighted_turned[:, block[b]], ident[:], is_transpose=True,
-                             start=False, stop=(b == 1))
+            nc.tensor.matmul(back[b][:, block[b]], weighted_turned[:, block[b]], ident[:], is_transpose=True,
+                             start=False, stop=True)
 
         result = keep.tile([P, S], F32, name="result")
         partial = keep.tile([P, HALF], F32, name="partial")
         upper_w = keep.tile([P, HALF], F32, name="upper_w")
-        nc.vector.scalar_tensor_tensor(partial[:], ss_by_p1[:, half[1]], 0.4, back[1][:, half[1]], MULT, ADD)
-        nc.vector.tensor_tensor(upper_w[:], fetched_upper[:], gate_sb[0][:, half[1]], MULT)
-        nc.vector.scalar_tensor_tensor(result[:, half[1]], upper_w[:], 0.4, partial[:], MULT, ADD)
+        nc.vector.scalar_tensor_tensor(partial[:], ss_by_p1[:, half[1]], 0.4, back[2][:, half[1]], MULT, ADD)
+        for b in (2, 3):
+            nc.vector.tensor_tensor(upper_w[:, block[b - 2]], fetched[1][:, block[b - 2]], gate_sb[0][:, block[b]], MULT)
+        for b in (2, 3):
+            nc.vector.scalar_tensor_tensor(result[:, block[b]], upper_w[:, block[b - 2]], 0.4, partial[:, block[b - 2]], MULT, ADD)
         nc.sync.dma_start(out=out[:, half[1]], in_=result[:, half[1]])
-        nc.vector.scalar_tensor_tensor(result[:, half[0]], ss_by_p1[:, half[0]], 0.4, back[0][:, half[0]], MULT, ADD)
+        for b in range(2):
+            nc.vector.scalar_tensor_tensor(result[:, block[b]], ss_by_p1[:, block[b]], 0.4, back[b][:, block[b]], MULT, ADD)
         nc.sync.dma_start(out=out[:, half[0]], in_=result[:, half[0]])

@@ -41,13 +41,11 @@ def tile_picked_ycns_two_p_kernel(tc, x_words, x_scales, w1, gate, goal, known, 
         for u in range(2):
             nc.vector.memset(table_scales[64 * u:64 * u + 24, :].bitcast(I32), 0)
             nc.gpsimd.memset(table_scales[64 * u + 32:64 * u + 64, :].bitcast(I32), 0)
-        w_rows = w1.rearrange("(p j) m -> p j m", j=PACK)
-        nc.sync.dma_start(out=w_raw[:, 0:3, :], in_=w_rows[:, 0:3, :])
+        nc.sync.dma_start(out=w_raw[:], in_=w1.rearrange("(p j) m -> p j m", j=PACK))
         for u in range(2):
             nc.sync.dma_start(out=table_scales[64 * u + 24:64 * u + 32, :].bitcast(I32), in_=rows[u])
         nc.sync.dma_start(offs_sb[:], offs)
         nc.sync.dma_start(pos_sb[0][:], pos1)
-        nc.sync.dma_start(out=w_raw[:, 3:4, :], in_=w_rows[:, 3:4, :])
         nc.sync.dma_start(out=table_words[:], in_=x_words[0].rearrange("p n t -> p (n t)").bitcast(I32))
         nc.sync.dma_start(pos_sb[1][:], pos2)
         nc.sync.dma_start(out=goal_sb[:], in_=goal)
@@ -72,8 +70,7 @@ def tile_picked_ycns_two_p_kernel(tc, x_words, x_scales, w1, gate, goal, known, 
         known_sb = late[:, 0, :]
         gate_sb = [late[:, 1, :], late[:, 2, :]]
         nc.sync.dma_start(out=known_sb, in_=known)
-        for d in (1, 0):
-            nc.sync.dma_start(out=gate_sb[d], in_=gate[d])
+        nc.sync.dma_start(out=late[:, 1:3, :], in_=gate.rearrange("d p s -> p d s"))
 
         half = [slice(h * HALF, (h + 1) * HALF) for h in range(2)]
         block = [slice(b * P, (b + 1) * P) for b in range(BLOCKS)]
@@ -99,7 +96,7 @@ def tile_picked_ycns_two_p_kernel(tc, x_words, x_scales, w1, gate, goal, known, 
                 nc.scalar.activation(p_sb[:, block[b]], logits[:, 0:P], TANH, scale=0.5)
         for part in (half[0], block[2], block[3]):
             nc.vector.scalar_tensor_tensor(miss[:, part], p_sb[:, part], -0.5, goal_sb[:, part], MULT, ADD)
-        for part in half:
+        for part in (half[0], block[2], block[3]):
             nc.vector.scalar_tensor_tensor(ee[:, part], miss[:, part], -0.5, known_sb[:, part], ADD, MULT)
 
         def fetch(window, d, cols, into):

@@ -82,7 +82,7 @@ def tile_picked_ycns_two_p_kernel(tc, x_words, x_scales, w1, gate, goal, known, 
             return listed[:, cols.start // STRIPE:cols.stop // STRIPE]
 
         p_sb = keep.tile([P, S], F32, name="p_sb")
-        miss = keep.tile([P, S], F32, name="miss")
+        miss = keep.tile([P, S], F32, name="miss", tag="miss_slot")
         ee = keep.tile([P, S + STRIPE], F32, name="ee")
         nc.vector.memset(ee[:, S:S + STRIPE], 0.0)
         for part in (half[0], block[2], block[3]):
@@ -108,7 +108,7 @@ def tile_picked_ycns_two_p_kernel(tc, x_words, x_scales, w1, gate, goal, known, 
         ss = keep.tile([P, S], F32, name="ss")
         second = keep.tile([P, S], F32, name="second")
         fetch_weighted(ee, 1, slice(0, S), second[:])
-        first = [keep.tile([P, HALF], F32, name="first%d" % h, tag="first_slot%d" % h) for h in range(2)]
+        first = [keep.tile([P, HALF], F32, name="first%d" % h) for h in range(2)]
         first_w = keep.tile([P, S], F32, name="first_w")
         for h in range(2):
             fetch(ee, 0, half[h], first[h][:])
@@ -117,7 +117,8 @@ def tile_picked_ycns_two_p_kernel(tc, x_words, x_scales, w1, gate, goal, known, 
         for h in range(2):
             nc.vector.tensor_tensor(ss[:, half[h]], first_w[:, half[h]], second[:, half[h]], ADD)
 
-        base_turned = keep.tile([P, S], F32, name="base_turned", tag="first_slot0")
+        turned_sb = keep.tile([P, S + 2], F32, name="turned_sb", tag="miss_slot")
+        base_turned, gate_column = turned_sb[:, 0:S], turned_sb[:, S:S + 2]
         for h in range(2):
             turned = bank("upright%d" % (2 + h), "base%d" % h)
             terms = [(term, b) for term in (p_sb, ee) for b in (2 * h, 2 * h + 1)]
@@ -125,11 +126,10 @@ def tile_picked_ycns_two_p_kernel(tc, x_words, x_scales, w1, gate, goal, known, 
                 nc.tensor.matmul(turned[:, block[b]], term[:, block[b]], ident[:], is_transpose=True,
                                  start=(i == 0), stop=(i == len(terms) - 1))
             nc.scalar.activation(base_turned[:, half[h]], turned[:, half[h]], COPY, scale=0.5, bias=0.5)
-        gate_turned = bank("upright2", "gate_turned")
+        gate_turned = bank("upright0", "gate_turned")
         for b in range(2):
             nc.tensor.transpose(gate_turned[:, block[b]], gate_sb[0][:, block[b]], ident[:])
-        gate_column = keep.tile([P, 2], F32, name="gate_column")
-        nc.scalar.activation(gate_column[:], gate_turned[:, 0:HALF:P], COPY, scale=0.4)
+        nc.scalar.activation(gate_column, gate_turned[:, 0:HALF:P], COPY, scale=0.4)
         back = [bank("back%d" % (i + 1), "back%d" % i) for i in range(3)]
         for b in range(BLOCKS):
             nc.tensor.matmul(back[min(b, 2)][:, block[b]], base_turned[:, block[b]], ident[:], is_transpose=True,

@@ -28,14 +28,15 @@ def tile_picked_ycns_two_p_kernel(tc, x_words, x_scales, w1, gate, goal, known, 
     nc = tc.nc
     with ExitStack() as ctx:
         keep = ctx.enter_context(tc.tile_pool(name="keep", bufs=1))
+        reused = ctx.enter_context(tc.tile_pool(name="reused", bufs=1))
         psum = ctx.enter_context(tc.psum_pool(name="psum", bufs=1))
 
         offs_sb = keep.tile([P, S // STRIPE], U16, name="offs_sb")
         pos_sb = [keep.tile([P, S // STRIPE], U16, name="pos%d_sb" % d) for d in range(2)]
         table_words = keep.tile([P, T], I32, name="table_words", align_bytes=64)
-        table_scales = keep.tile([P, T], U8, name="table_scales", tag="scales_slot", align_bytes=64)
+        table_scales = reused.tile([P, T], U8, name="table_scales", offset=0, align_bytes=64)
         w_raw = keep.tile([P, PACK, N], F32, name="w_raw")
-        goal_sb = keep.tile([P, S], F32, name="goal_sb")
+        known_sb = keep.tile([P, S], F32, name="known_sb")
 
         rows = x_scales[0].bitcast(I32).rearrange("(e u r) c -> u r e c", e=2, u=2)
         for u in range(2):
@@ -48,13 +49,13 @@ def tile_picked_ycns_two_p_kernel(tc, x_words, x_scales, w1, gate, goal, known, 
         nc.sync.dma_start(pos_sb[0][:], pos1)
         nc.sync.dma_start(out=table_words[:], in_=x_words[0].rearrange("p n t -> p (n t)").bitcast(I32))
         nc.sync.dma_start(pos_sb[1][:], pos2)
-        nc.sync.dma_start(out=goal_sb[:], in_=goal)
+        nc.sync.dma_start(out=known_sb[:], in_=known)
         ident = keep.tile([P, P], F32, name="ident")
         make_identity(nc, ident[:])
 
         picked_scales = keep.tile([P, S], U8, name="picked_scales", align_bytes=64)
-        w_grouped = keep.tile([P, N, PACK], BF16, name="w_grouped", tag="grouped_slot", align_bytes=64)
-        nc.vector.tensor_copy(out=w_grouped[:], in_=w_raw[:].rearrange("p j m -> p m j"))
+        w_grouped = keep.tile([P, N, PACK], BF16, name="w_grouped", tag="picked_words0", align_bytes=64)
+        nc.scalar.activation(w_grouped[:], w_raw[:].rearrange("p j m -> p m j"), COPY)
         spread = keep.tile([P, S], U8, name="spread", align_bytes=64)
         for h in range(2):
             cols = slice(h * HALF, (h + 1) * HALF)
@@ -62,14 +63,14 @@ def tile_picked_ycns_two_p_kernel(tc, x_words, x_scales, w1, gate, goal, known, 
             for e in range(2):
                 nc.sync.dma_start(out=picked_scales[64 * e:64 * e + 64, cols].bitcast(I32), in_=spread[e:P:2, cols].bitcast(I32))
 
-        w_codes = keep.tile([P, N], U32, name="w_codes", tag="scales_slot", align_bytes=64)
+        w_codes = reused.tile([P, N], U32, name="w_codes", offset=0, align_bytes=64)
         w_scales = keep.tile([P, N], U8, name="w_scales", align_bytes=64)
         nc.vector.quantize_mx(out=w_codes[:].bitcast(FP8X4), scales=w_scales[:],
                               in_=w_grouped[:].rearrange("p m j -> p (m j)"))
-        late = keep.tile([P, 3, S], F32, name="late", tag="grouped_slot", align_bytes=64)
-        known_sb = late[:, 0, :]
+        late = reused.tile([P, 3, S], F32, name="late", offset=4 * N, align_bytes=64)
+        goal_sb = late[:, 0, :]
         gate_sb = [late[:, 1, :], late[:, 2, :]]
-        nc.sync.dma_start(out=known_sb, in_=known)
+        nc.sync.dma_start(out=goal_sb, in_=goal)
         nc.sync.dma_start(out=late[:, 1:3, :], in_=gate.rearrange("d p s -> p d s"))
 
         half = [slice(h * HALF, (h + 1) * HALF) for h in range(2)]
@@ -86,7 +87,7 @@ def tile_picked_ycns_two_p_kernel(tc, x_words, x_scales, w1, gate, goal, known, 
         ee = keep.tile([P, S + STRIPE], F32, name="ee")
         nc.vector.memset(ee[:, S:S + STRIPE], 0.0)
         for part in (half[0], block[2], block[3]):
-            words = keep.tile([P, part.stop - part.start], U32, name="picked_words%d" % part.start, align_bytes=64)
+            words = keep.tile([P, part.stop - part.start], U32, name="picked_words%d" % part.start, tag="picked_words%d" % part.start, align_bytes=64)
             nc.vector.tensor_copy(words[:], table_words[:].bitcast(U32).indirect(entries(offs_sb, part)))
             for b in range(part.start // P, part.stop // P):
                 logits = bank("upright%d" % b, "logits%d" % b)
@@ -94,9 +95,11 @@ def tile_picked_ycns_two_p_kernel(tc, x_words, x_scales, w1, gate, goal, known, 
                                     rhs=words[:, b * P - part.start:(b + 1) * P - part.start].bitcast(FP8X4),
                                     rhs_scale=picked_scales[12:P, block[b]], start=True, stop=True)
                 nc.scalar.activation(p_sb[:, block[b]], logits[:, 0:P], TANH, scale=0.5)
-        for part in (half[0], block[2], block[3]):
-            nc.vector.scalar_tensor_tensor(miss[:, part], p_sb[:, part], -0.5, goal_sb[:, part], MULT, ADD)
-        for part in (half[0], block[2], block[3]):
+        for b in range(BLOCKS):
+            if b == BLOCKS - 1:
+                nc.vector.scalar_tensor_tensor(ee[:, block[0]], miss[:, block[0]], -0.5, known_sb[:, block[0]], ADD, MULT)
+            nc.vector.scalar_tensor_tensor(miss[:, block[b]], p_sb[:, block[b]], -0.5, goal_sb[:, block[b]], MULT, ADD)
+        for part in (slice(P, 3 * P), block[3]):
             nc.vector.scalar_tensor_tensor(ee[:, part], miss[:, part], -0.5, known_sb[:, part], ADD, MULT)
 
         def fetch(window, d, cols, into):

@@ -9,6 +9,9 @@ PACK = 4
 STRIPE = 16
 HALF = S // 2
 BLOCKS = S // P
+PLANE = 12
+LOADED = 2 * PLANE
+DAMP = 0.8 * 0.5
 FLOPS = 2 * K * N * S
 
 F32 = mybir.dt.float32
@@ -36,20 +39,20 @@ def tile_picked_ycns_two_p_kernel(tc, x_words, x_scales, w1, gate, goal, known, 
         table_words = keep.tile([P, T], I32, name="table_words", align_bytes=64)
         table_scales = reused.tile([P, T], U8, name="table_scales", offset=0, align_bytes=64)
         w_raw = keep.tile([P, PACK, N], F32, name="w_raw")
-        known_sb = keep.tile([P, S], F32, name="known_sb")
+        goal_sb = keep.tile([P, S], F32, name="goal_sb")
 
         rows = x_scales[0].bitcast(I32).rearrange("(e u r) c -> u r e c", e=2, u=2)
         for u in range(2):
-            nc.vector.memset(table_scales[64 * u:64 * u + 24, :].bitcast(I32), 0)
+            nc.vector.memset(table_scales[64 * u:64 * u + LOADED, :].bitcast(I32), 0)
             nc.gpsimd.memset(table_scales[64 * u + 32:64 * u + 64, :].bitcast(I32), 0)
         nc.sync.dma_start(out=w_raw[:], in_=w1.rearrange("(p j) m -> p j m", j=PACK))
         for u in range(2):
-            nc.sync.dma_start(out=table_scales[64 * u + 24:64 * u + 32, :].bitcast(I32), in_=rows[u])
+            nc.sync.dma_start(out=table_scales[64 * u + LOADED:64 * u + 32, :].bitcast(I32), in_=rows[u])
         nc.sync.dma_start(offs_sb[:], offs)
         nc.sync.dma_start(pos_sb[0][:], pos1)
         nc.sync.dma_start(out=table_words[:], in_=x_words[0].rearrange("p n t -> p (n t)").bitcast(I32))
         nc.sync.dma_start(pos_sb[1][:], pos2)
-        nc.sync.dma_start(out=known_sb[:], in_=known)
+        nc.sync.dma_start(out=goal_sb[:], in_=goal)
         ident = keep.tile([P, P], F32, name="ident")
         make_identity(nc, ident[:])
 
@@ -60,17 +63,17 @@ def tile_picked_ycns_two_p_kernel(tc, x_words, x_scales, w1, gate, goal, known, 
         for h in range(2):
             cols = slice(h * HALF, (h + 1) * HALF)
             nc.vector.tensor_copy(spread[:, cols], table_scales[:].indirect(offs_sb[:, h * HALF // STRIPE:(h + 1) * HALF // STRIPE]))
-            for e in range(2):
-                nc.sync.dma_start(out=picked_scales[64 * e:64 * e + 64, cols].bitcast(I32), in_=spread[e:P:2, cols].bitcast(I32))
+            for e, queue in enumerate((nc.sync, nc.scalar)):
+                queue.dma_start(out=picked_scales[64 * e:64 * e + 64, cols].bitcast(I32), in_=spread[e:P:2, cols].bitcast(I32))
 
         w_codes = reused.tile([P, N], U32, name="w_codes", offset=0, align_bytes=64)
         w_scales = keep.tile([P, N], U8, name="w_scales", align_bytes=64)
         nc.vector.quantize_mx(out=w_codes[:].bitcast(FP8X4), scales=w_scales[:],
                               in_=w_grouped[:].rearrange("p m j -> p (m j)"))
         late = reused.tile([P, 3, S], F32, name="late", offset=4 * N, align_bytes=64)
-        goal_sb = late[:, 0, :]
+        known_sb = late[:, 0, :]
         gate_sb = [late[:, 1, :], late[:, 2, :]]
-        nc.sync.dma_start(out=goal_sb, in_=goal)
+        nc.sync.dma_start(out=known_sb, in_=known)
         nc.sync.dma_start(out=late[:, 1:3, :], in_=gate.rearrange("d p s -> p d s"))
 
         half = [slice(h * HALF, (h + 1) * HALF) for h in range(2)]
@@ -82,23 +85,24 @@ def tile_picked_ycns_two_p_kernel(tc, x_words, x_scales, w1, gate, goal, known, 
         def entries(listed, cols):
             return listed[:, cols.start // STRIPE:cols.stop // STRIPE]
 
-        p_sb = keep.tile([P, S], F32, name="p_sb")
+        tanh_sb = keep.tile([P, S], F32, name="tanh_sb")
         miss = keep.tile([P, S], F32, name="miss", tag="miss_slot")
         ee = keep.tile([P, S + STRIPE], F32, name="ee")
         nc.vector.memset(ee[:, S:S + STRIPE], 0.0)
         for part in (half[0], block[2], block[3]):
-            words = keep.tile([P, part.stop - part.start], U32, name="picked_words%d" % part.start, tag="picked_words%d" % part.start, align_bytes=64)
+            words = keep.tile([P, part.stop - part.start], U32, name="picked_words%d" % part.start,
+                              tag="picked_words%d" % part.start, align_bytes=64)
             nc.vector.tensor_copy(words[:], table_words[:].bitcast(U32).indirect(entries(offs_sb, part)))
             for b in range(part.start // P, part.stop // P):
                 logits = bank("upright%d" % b, "logits%d" % b)
                 nc.tensor.matmul_mx(out=logits[:, 0:P], lhsT=w_codes[:].bitcast(FP8X4), lhsT_scale=w_scales[:],
                                     rhs=words[:, b * P - part.start:(b + 1) * P - part.start].bitcast(FP8X4),
-                                    rhs_scale=picked_scales[12:P, block[b]], start=True, stop=True)
-                nc.scalar.activation(p_sb[:, block[b]], logits[:, 0:P], TANH, scale=0.5)
+                                    rhs_scale=picked_scales[PLANE:P, block[b]], start=True, stop=True)
+                nc.scalar.activation(tanh_sb[:, block[b]], logits[:, 0:P], TANH, scale=0.5)
         for b in range(BLOCKS):
             if b == BLOCKS - 1:
                 nc.vector.scalar_tensor_tensor(ee[:, block[0]], miss[:, block[0]], -0.5, known_sb[:, block[0]], ADD, MULT)
-            nc.vector.scalar_tensor_tensor(miss[:, block[b]], p_sb[:, block[b]], -0.5, goal_sb[:, block[b]], MULT, ADD)
+            nc.vector.scalar_tensor_tensor(miss[:, block[b]], tanh_sb[:, block[b]], -0.5, goal_sb[:, block[b]], MULT, ADD)
         for part in (slice(P, 3 * P), block[3]):
             nc.vector.scalar_tensor_tensor(ee[:, part], miss[:, part], -0.5, known_sb[:, part], ADD, MULT)
 
@@ -124,7 +128,7 @@ def tile_picked_ycns_two_p_kernel(tc, x_words, x_scales, w1, gate, goal, known, 
         base_turned, gate_column = turned_sb[:, 0:S], turned_sb[:, S:S + 2]
         for h in range(2):
             turned = bank("upright%d" % (2 + h), "base%d" % h)
-            terms = [(term, b) for term in (p_sb, ee) for b in (2 * h, 2 * h + 1)]
+            terms = [(term, b) for term in (tanh_sb, ee) for b in (2 * h, 2 * h + 1)]
             for i, (term, b) in enumerate(terms):
                 nc.tensor.matmul(turned[:, block[b]], term[:, block[b]], ident[:], is_transpose=True,
                                  start=(i == 0), stop=(i == len(terms) - 1))
@@ -132,7 +136,7 @@ def tile_picked_ycns_two_p_kernel(tc, x_words, x_scales, w1, gate, goal, known, 
         gate_turned = bank("upright0", "gate_turned")
         for b in range(2):
             nc.tensor.transpose(gate_turned[:, block[b]], gate_sb[0][:, block[b]], ident[:])
-        nc.scalar.activation(gate_column, gate_turned[:, 0:HALF:P], COPY, scale=0.4)
+        nc.scalar.activation(gate_column, gate_turned[:, 0:HALF:P], COPY, scale=DAMP)
         back = [bank("back%d" % (i + 1), "back%d" % i) for i in range(3)]
         for b in range(BLOCKS):
             nc.tensor.matmul(back[min(b, 2)][:, block[b]], base_turned[:, block[b]], ident[:], is_transpose=True,
@@ -156,12 +160,12 @@ def tile_picked_ycns_two_p_kernel(tc, x_words, x_scales, w1, gate, goal, known, 
         result = keep.tile([P, S], F32, name="result")
         partial = keep.tile([P, HALF], F32, name="partial")
         upper_w = keep.tile([P, HALF], F32, name="upper_w")
-        nc.vector.scalar_tensor_tensor(partial[:], ss_by_p1[:, half[1]], 0.4, back[2][:, half[1]], MULT, ADD)
+        nc.vector.scalar_tensor_tensor(partial[:], ss_by_p1[:, half[1]], DAMP, back[2][:, half[1]], MULT, ADD)
         for b in (2, 3):
             nc.vector.tensor_tensor(upper_w[:, block[b - 2]], fetched[1][:, block[b - 2]], gate_sb[0][:, block[b]], MULT)
         for b in (2, 3):
-            nc.vector.scalar_tensor_tensor(result[:, block[b]], upper_w[:, block[b - 2]], 0.4, partial[:, block[b - 2]], MULT, ADD)
+            nc.vector.scalar_tensor_tensor(result[:, block[b]], upper_w[:, block[b - 2]], DAMP, partial[:, block[b - 2]], MULT, ADD)
         nc.sync.dma_start(out=out[:, half[1]], in_=result[:, half[1]])
         for b in range(2):
-            nc.vector.scalar_tensor_tensor(result[:, block[b]], ss_by_p1[:, block[b]], 0.4, back[b][:, block[b]], MULT, ADD)
+            nc.vector.scalar_tensor_tensor(result[:, block[b]], ss_by_p1[:, block[b]], DAMP, back[b][:, block[b]], MULT, ADD)
         nc.sync.dma_start(out=out[:, half[0]], in_=result[:, half[0]])

@@ -11,6 +11,7 @@ HALF = S // 2
 BLOCKS = S // P
 PLANE = 12
 LOADED = 2 * PLANE
+ROW_ALIGN = 256
 DAMP = 0.8 * 0.5
 FLOPS = 2 * K * N * S
 
@@ -36,10 +37,10 @@ def tile_picked_ycns_two_p_kernel(tc, x_words, x_scales, w1, gate, goal, known, 
 
         offs_sb = keep.tile([P, S // STRIPE], U16, name="offs_sb")
         pos_sb = [keep.tile([P, S // STRIPE], U16, name="pos%d_sb" % d) for d in range(2)]
-        table_words = keep.tile([P, T], I32, name="table_words", align_bytes=64)
-        table_scales = reused.tile([P, T], U8, name="table_scales", offset=0, align_bytes=64)
-        w_raw = keep.tile([P, PACK, N], F32, name="w_raw")
-        goal_sb = keep.tile([P, S], F32, name="goal_sb")
+        table_words = keep.tile([P, T], I32, name="table_words", align_bytes=ROW_ALIGN)
+        table_scales = reused.tile([P, T], U8, name="table_scales", offset=0, align_bytes=ROW_ALIGN)
+        w_raw = keep.tile([P, PACK, N], F32, name="w_raw", align_bytes=ROW_ALIGN)
+        goal_sb = keep.tile([P, S], F32, name="goal_sb", align_bytes=ROW_ALIGN)
 
         rows = x_scales[0].bitcast(I32).rearrange("(e u r) c -> u r e c", e=2, u=2)
         for u in range(2):
@@ -56,10 +57,10 @@ def tile_picked_ycns_two_p_kernel(tc, x_words, x_scales, w1, gate, goal, known, 
         ident = keep.tile([P, P], F32, name="ident")
         make_identity(nc, ident[:])
 
-        picked_scales = keep.tile([P, S], U8, name="picked_scales", align_bytes=64)
+        picked_scales = keep.tile([P, S], U8, name="picked_scales", align_bytes=ROW_ALIGN)
         w_grouped = keep.tile([P, N, PACK], BF16, name="w_grouped", tag="picked_words0", align_bytes=64)
         nc.scalar.activation(w_grouped[:], w_raw[:].rearrange("p j m -> p m j"), COPY)
-        spread = keep.tile([P, S], U8, name="spread", align_bytes=64)
+        spread = keep.tile([P, S], U8, name="spread", align_bytes=ROW_ALIGN)
         for h in range(2):
             cols = slice(h * HALF, (h + 1) * HALF)
             nc.vector.tensor_copy(spread[:, cols], table_scales[:].indirect(offs_sb[:, h * HALF // STRIPE:(h + 1) * HALF // STRIPE]))
@@ -70,7 +71,7 @@ def tile_picked_ycns_two_p_kernel(tc, x_words, x_scales, w1, gate, goal, known, 
         w_scales = keep.tile([P, N], U8, name="w_scales", align_bytes=64)
         nc.vector.quantize_mx(out=w_codes[:].bitcast(FP8X4), scales=w_scales[:],
                               in_=w_grouped[:].rearrange("p m j -> p (m j)"))
-        late = reused.tile([P, 3, S], F32, name="late", offset=4 * N, align_bytes=64)
+        late = reused.tile([P, 3, S], F32, name="late", offset=4 * N, align_bytes=ROW_ALIGN)
         known_sb = late[:, 0, :]
         gate_sb = [late[:, 1, :], late[:, 2, :]]
         nc.sync.dma_start(out=known_sb, in_=known)
@@ -157,7 +158,7 @@ def tile_picked_ycns_two_p_kernel(tc, x_words, x_scales, w1, gate, goal, known, 
             nc.tensor.matmul(back[b][:, block[b]], weighted_turned[:, block[b]], ident[:], is_transpose=True,
                              start=False, stop=True)
 
-        result = keep.tile([P, S], F32, name="result")
+        result = keep.tile([P, S], F32, name="result", align_bytes=ROW_ALIGN)
         partial = keep.tile([P, HALF], F32, name="partial")
         upper_w = keep.tile([P, HALF], F32, name="upper_w")
         nc.vector.scalar_tensor_tensor(partial[:], ss_by_p1[:, half[1]], DAMP, back[2][:, half[1]], MULT, ADD)

@@ -45,7 +45,7 @@ def tile_picked_ycns_two_p_kernel(tc, x_words, x_scales, w1, gate, goal, known, 
         rows = x_scales[0].bitcast(I32).rearrange("(e u r) c -> u r e c", e=2, u=2)
         for u in range(2):
             nc.vector.memset(table_scales[64 * u:64 * u + LOADED, :].bitcast(I32), 0)
-            nc.gpsimd.memset(table_scales[64 * u + 32:64 * u + 64, :].bitcast(I32), 0)
+            nc.vector.memset(table_scales[64 * u + 32:64 * u + 64, :].bitcast(I32), 0)
         nc.sync.dma_start(out=w_raw[:], in_=w1.rearrange("(p j) m -> p j m", j=PACK))
         for u in range(2):
             nc.sync.dma_start(out=table_scales[64 * u + LOADED:64 * u + 32, :].bitcast(I32), in_=rows[u])

from contextlib import ExitStack

import concourse.mybir as mybir
from concourse.masks import make_identity

K, T, S, N = 512, 2048, 512, 128
P = 128
PACK = 4
STRIPE = 16
HALF = S // 2
BLOCKS = S // P
PLANE = 12
LOADED = 2 * PLANE
ROW_ALIGN = 256
DAMP = 0.8 * 0.5
FLOPS = 2 * K * N * S

F32 = mybir.dt.float32
BF16 = mybir.dt.bfloat16
I32 = mybir.dt.int32
U32 = mybir.dt.uint32
U16 = mybir.dt.uint16
U8 = mybir.dt.uint8
FP8X4 = mybir.dt.float8_e4m3fn_x4
MULT = mybir.AluOpType.mult
ADD = mybir.AluOpType.add
TANH = mybir.ActivationFunctionType.Tanh
COPY = mybir.ActivationFunctionType.Copy


def tile_picked_ycns_two_p_kernel(tc, x_words, x_scales, w1, gate, goal, known, offs, pos1, pos2, out):
    nc = tc.nc
    with ExitStack() as ctx:
        keep = ctx.enter_context(tc.tile_pool(name="keep", bufs=1))
        reused = ctx.enter_context(tc.tile_pool(name="reused", bufs=1))
        psum = ctx.enter_context(tc.psum_pool(name="psum", bufs=1))

        offs_sb = keep.tile([P, S // STRIPE], U16, name="offs_sb")
        pos_sb = [keep.tile([P, S // STRIPE], U16, name="pos%d_sb" % d) for d in range(2)]
        table_words = keep.tile([P, T], I32, name="table_words", align_bytes=ROW_ALIGN)
        table_scales = reused.tile([P, T], U8, name="table_scales", offset=0, align_bytes=ROW_ALIGN)
        w_raw = keep.tile([P, PACK, N], F32, name="w_raw", align_bytes=ROW_ALIGN)
        goal_sb = keep.tile([P, S], F32, name="goal_sb", align_bytes=ROW_ALIGN)

        rows = x_scales[0].bitcast(I32).rearrange("(e u r) c -> u r e c", e=2, u=2)
        for u in range(2):
            nc.vector.memset(table_scales[64 * u:64 * u + LOADED, :].bitcast(I32), 0)
            nc.vector.memset(table_scales[64 * u + 32:64 * u + 64, :].bitcast(I32), 0)
        nc.sync.dma_start(out=w_raw[:], in_=w1.rearrange("(p j) m -> p j m", j=PACK))
        for u in range(2):
            nc.sync.dma_start(out=table_scales[64 * u + LOADED:64 * u + 32, :].bitcast(I32), in_=rows[u])
        nc.sync.dma_start(offs_sb[:], offs)
        nc.sync.dma_start(pos_sb[0][:], pos1)
        nc.sync.dma_start(out=table_words[:], in_=x_words[0].rearrange("p n t -> p (n t)").bitcast(I32))
        nc.sync.dma_start(pos_sb[1][:], pos2)
        nc.sync.dma_start(out=goal_sb[:], in_=goal)
        ident = keep.tile([P, P], F32, name="ident")
        make_identity(nc, ident[:])

        picked_scales = keep.tile([P, S], U8, name="picked_scales", align_bytes=ROW_ALIGN)
        w_grouped = keep.tile([P, N, PACK], BF16, name="w_grouped", tag="picked_words0", align_bytes=64)
        nc.scalar.activation(w_grouped[:], w_raw[:].rearrange("p j m -> p m j"), COPY)
        spread = keep.tile([P, S], U8, name="spread", align_bytes=ROW_ALIGN)
        for h in range(2):
            cols = slice(h * HALF, (h + 1) * HALF)
            nc.vector.tensor_copy(spread[:, cols], table_scales[:].indirect(offs_sb[:, h * HALF // STRIPE:(h + 1) * HALF // STRIPE]))
            for e, queue in enumerate((nc.sync, nc.scalar)):
                queue.dma_start(out=picked_scales[64 * e:64 * e + 64, cols].bitcast(I32), in_=spread[e:P:2, cols].bitcast(I32))

        w_codes = reused.tile([P, N], U32, name="w_codes", offset=0, align_bytes=64)
        w_scales = keep.tile([P, N], U8, name="w_scales", align_bytes=64)
        nc.vector.quantize_mx(out=w_codes[:].bitcast(FP8X4), scales=w_scales[:],
                              in_=w_grouped[:].rearrange("p m j -> p (m j)"))
        late = reused.tile([P, 3, S], F32, name="late", offset=4 * N, align_bytes=ROW_ALIGN)
        known_sb = late[:, 0, :]
        gate_sb = [late[:, 1, :], late[:, 2, :]]
        nc.sync.dma_start(out=known_sb, in_=known)
        nc.sync.dma_start(out=late[:, 1:3, :], in_=gate.rearrange("d p s -> p d s"))

        half = [slice(h * HALF, (h + 1) * HALF) for h in range(2)]
        block = [slice(b * P, (b + 1) * P) for b in range(BLOCKS)]

        def bank(tag, name):
            return psum.tile([P, S], F32, name=name, tag=tag)

        def entries(listed, cols):
            return listed[:, cols.start // STRIPE:cols.stop // STRIPE]

        tanh_sb = keep.tile([P, S], F32, name="tanh_sb")
        miss = keep.tile([P, S], F32, name="miss", tag="miss_slot")
        ee = keep.tile([P, S + STRIPE], F32, name="ee")
        nc.vector.memset(ee[:, S:S + STRIPE], 0.0)
        for part in (half[0], block[2], block[3]):
            words = keep.tile([P, part.stop - part.start], U32, name="picked_words%d" % part.start,
                              tag="picked_words%d" % part.start, align_bytes=64)
            nc.vector.tensor_copy(words[:], table_words[:].bitcast(U32).indirect(entries(offs_sb, part)))
            for b in range(part.start // P, part.stop // P):
                logits = bank("upright%d" % b, "logits%d" % b)
                nc.tensor.matmul_mx(out=logits[:, 0:P], lhsT=w_codes[:].bitcast(FP8X4), lhsT_scale=w_scales[:],
                                    rhs=words[:, b * P - part.start:(b + 1) * P - part.start].bitcast(FP8X4),
                                    rhs_scale=picked_scales[PLANE:P, block[b]], start=True, stop=True)
                nc.scalar.activation(tanh_sb[:, block[b]], logits[:, 0:P], TANH, scale=0.5)
        for b in range(BLOCKS):
            if b == BLOCKS - 1:
                nc.vector.scalar_tensor_tensor(ee[:, block[0]], miss[:, block[0]], -0.5, known_sb[:, block[0]], ADD, MULT)
            nc.vector.scalar_tensor_tensor(miss[:, block[b]], tanh_sb[:, block[b]], -0.5, goal_sb[:, block[b]], MULT, ADD)
        for part in (slice(P, 3 * P), block[3]):
            nc.vector.scalar_tensor_tensor(ee[:, part], miss[:, part], -0.5, known_sb[:, part], ADD, MULT)

        def fetch(window, d, cols, into):
            nc.scalar.activation(into, window[:].indirect(entries(pos_sb[d], cols)), COPY)

        def fetch_weighted(window, d, cols, into):
            nc.vector.tensor_tensor(into, window[:].indirect(entries(pos_sb[d], cols)), gate_sb[d][:, cols], MULT)

        ss = keep.tile([P, S], F32, name="ss")
        second = keep.tile([P, S], F32, name="second")
        fetch_weighted(ee, 1, slice(0, S), second[:])
        first = [keep.tile([P, HALF], F32, name="first%d" % h) for h in range(2)]
        first_w = keep.tile([P, S], F32, name="first_w")
        for h in range(2):
            fetch(ee, 0, half[h], first[h][:])
        for h in range(2):
            nc.vector.tensor_tensor(first_w[:, half[h]], first[h][:], gate_sb[0][:, half[h]], MULT)
        for h in range(2):
            nc.vector.tensor_tensor(ss[:, half[h]], first_w[:, half[h]], second[:, half[h]], ADD)

        turned_sb = keep.tile([P, S + 2], F32, name="turned_sb", tag="miss_slot")
        base_turned, gate_column = turned_sb[:, 0:S], turned_sb[:, S:S + 2]
        for h in range(2):
            turned = bank("upright%d" % (2 + h), "base%d" % h)
            terms = [(term, b) for term in (tanh_sb, ee) for b in (2 * h, 2 * h + 1)]
            for i, (term, b) in enumerate(terms):
                nc.tensor.matmul(turned[:, block[b]], term[:, block[b]], ident[:], is_transpose=True,
                                 start=(i == 0), stop=(i == len(terms) - 1))
            nc.scalar.activation(base_turned[:, half[h]], turned[:, half[h]], COPY, scale=0.5, bias=0.5)
        gate_turned = bank("upright0", "gate_turned")
        for b in range(2):
            nc.tensor.transpose(gate_turned[:, block[b]], gate_sb[0][:, block[b]], ident[:])
        nc.scalar.activation(gate_column, gate_turned[:, 0:HALF:P], COPY, scale=DAMP)
        back = [bank("back%d" % (i + 1), "back%d" % i) for i in range(3)]
        for b in range(BLOCKS):
            nc.tensor.matmul(back[min(b, 2)][:, block[b]], base_turned[:, block[b]], ident[:], is_transpose=True,
                             start=(b != 3), stop=(b == 3))

        weighted_turned = keep.tile([P, HALF], F32, name="weighted_turned")
        fetched = [keep.tile([P, HALF], F32, name="fetched%d" % h) for h in range(2)]
        for b in range(2):
            fetch(ss, 0, block[b], fetched[0][:, block[b]])
        fetch(ss, 0, half[1], fetched[1][:])
        ss_by_p1 = keep.tile([P, S], F32, name="ss_by_p1")
        for h in (1, 0):
            fetch_weighted(ss, 1, half[h], ss_by_p1[:, half[h]])
        for b in range(2):
            turned = bank(("upright1", "back0")[b], "fetched_turned%d" % b)
            nc.tensor.transpose(turned[:, 0:P], fetched[0][:, block[b]], ident[:])
            nc.scalar.activation(weighted_turned[:, block[b]], turned[:, 0:P], COPY, scale=gate_column[:, b:b + 1])
            nc.tensor.matmul(back[b][:, block[b]], weighted_turned[:, block[b]], ident[:], is_transpose=True,
                             start=False, stop=True)

        result = keep.tile([P, S], F32, name="result", align_bytes=ROW_ALIGN)
        partial = keep.tile([P, HALF], F32, name="partial")
        upper_w = keep.tile([P, HALF], F32, name="upper_w")
        nc.vector.scalar_tensor_tensor(partial[:], ss_by_p1[:, half[1]], DAMP, back[2][:, half[1]], MULT, ADD)
        for b in (2, 3):
            nc.vector.tensor_tensor(upper_w[:, block[b - 2]], fetched[1][:, block[b - 2]], gate_sb[0][:, block[b]], MULT)
        for b in (2, 3):
            nc.vector.scalar_tensor_tensor(result[:, block[b]], upper_w[:, block[b - 2]], DAMP, partial[:, block[b - 2]], MULT, ADD)
        nc.sync.dma_start(out=out[:, half[1]], in_=result[:, half[1]])
        for b in range(2):
            nc.vector.scalar_tensor_tensor(result[:, block[b]], ss_by_p1[:, block[b]], DAMP, back[b][:, block[b]], MULT, ADD)
        nc.sync.dma_start(out=out[:, half[0]], in_=result[:, half[0]])
